import numpy as np
import ml_dtypes


def mxq(x, axis, fmt="e4m3"):
    dtype, down = {"e4m3": (ml_dtypes.float8_e4m3fn, 7), "e5m2": (ml_dtypes.float8_e5m2, 14)}[fmt]
    v = np.moveaxis(np.asarray(x, np.float32).astype(ml_dtypes.bfloat16).astype(np.float64), axis, -1)
    blocks = v.reshape(v.shape[:-1] + (-1, 32))
    amax = np.abs(blocks).max(-1, keepdims=True)
    byte = np.maximum(np.where(amax > 0, np.frexp(amax)[1] - 1 + 127, 0) - down, 1)
    scale = np.exp2(byte - 127.0)
    codes = (blocks / scale).astype(np.float32).astype(dtype).astype(np.float64)
    return np.moveaxis((codes * scale).reshape(v.shape), -1, axis)


WIDE = False


def mx_kscale(k):
    if not WIDE:
        return np.ones(k)
    levels = np.array([10, -10, 5, -5, 0])
    if k % 512:
        return np.exp2(np.random.permutation(np.resize(levels, k // 32))).repeat(32)
    a = np.empty((k // 512, 16))
    for p in range(k // 512):
        a[p, :8] = np.random.permutation(np.resize(levels, 8))
        for g in range(8):
            far = levels[np.abs(levels - a[p, g]) >= 10]
            a[p, g + 8] = far[np.random.randint(len(far))]
    return np.exp2(a.ravel()).repeat(32)


BF16 = ml_dtypes.bfloat16


def bf(x):
    return np.asarray(x, np.float32).astype(BF16)


def f64(x):
    return np.asarray(x).astype(np.float64)


E2M1 = np.array([0.0, 0.5, 1.0, 1.5, 2.0, 3.0, 4.0, 6.0, -0.0, -0.5, -1.0, -1.5, -2.0, -3.0, -4.0, -6.0])


def pack_weight(w, fmt):
    k, n = w.shape
    w = f64(bf(w)).reshape(k // 32, 32, n)
    amax = np.abs(w).max(1)
    if fmt == "e4m3":
        byte = np.frexp(amax)[1] - 1 + 127 - 7
    else:
        mant, ex = np.frexp(amax / 6.0)
        byte = np.where(mant > 0.5, ex, ex - 1) + 127
    byte = np.clip(np.where(amax > 0, byte, 1), 1, 254)
    scaled = (w * np.exp2(127.0 - byte)[:, None, :]).reshape(k, n).astype(np.float32)
    by_word = np.ascontiguousarray(scaled.reshape(k // 512, 128, 4, n).transpose(0, 1, 3, 2))
    if fmt == "e4m3":
        words = by_word.astype(ml_dtypes.float8_e4m3fn).view(np.uint8)
    else:
        c = by_word.astype(ml_dtypes.float4_e2m1fn).view(np.uint8) & 0xF
        words = c[..., 0::2] | (c[..., 1::2] << 4)
    return np.ascontiguousarray(words), np.ascontiguousarray(byte.astype(np.uint8).reshape(k // 512, 16, n))


def unpack_weight(words, scales, fmt):
    g, p, n, _ = words.shape
    if fmt == "e4m3":
        vals = np.ascontiguousarray(words).view(ml_dtypes.float8_e4m3fn).astype(np.float64)
    else:
        nib = np.empty((g, p, n, 4), np.uint8)
        nib[..., 0::2] = words & 0xF
        nib[..., 1::2] = words >> 4
        vals = E2M1[nib]
    vals = vals * np.repeat(np.exp2(scales.astype(np.float64) - 127.0), 8, axis=1)[..., None]
    return vals.transpose(0, 1, 3, 2).reshape(g * 512, n)
def pack4(w):
    words, scales = pack_weight(w, "e2m1")
    return words.reshape(words.shape[0], 128, -1), scales


def unpack4(words, scales):
    return unpack_weight(words.reshape(words.shape[0], 128, -1, 2), scales, "e2m1")


def planes(Y):
    n, m = Y.shape
    b = f64(bf(Y)).reshape(n // 32, 32, m)
    amax = np.abs(b).max(1)
    byte = np.clip(np.where(amax > 0, np.frexp(amax)[1] - 1 + 127 - 7, 1), 1, 254)
    codes = (b * np.exp2(127.0 - byte)[:, None, :]).reshape(n, m).astype(np.float32).astype(ml_dtypes.float8_e4m3fn).view(np.uint8)
    words = codes.reshape(n // 512, 128, 4, m).transpose(0, 1, 3, 2)
    return np.ascontiguousarray(words), np.ascontiguousarray(byte.astype(np.uint8).reshape(n // 512, 16, m))


B, S, D, M = 8, 512, 512, 256


def stable_softmax(x, axis):
    ex = np.exp(x - np.max(x, axis=axis, keepdims=True))
    return ex / np.sum(ex, axis=axis, keepdims=True)


def setup_inputs():
    s, r, t = mx_kscale(D), mx_kscale(D), mx_kscale(S)
    h = np.random.standard_normal((B, S, D)) * s
    w1 = np.random.standard_normal((D, M)) / np.sqrt(D) / s[:, None]
    tb = np.random.uniform(-2.5, 0.0, (B, S))
    g = np.random.standard_normal((B, S)) * t
    e = np.random.standard_normal((B, S, D)) * r / t[:, None]
    ws = np.random.standard_normal((D, D)) / np.sqrt(D) / r[:, None]
    c = np.random.standard_normal((B, D))
    w1_words, w1_scales = pack4(w1)
    ws_words, ws_scales = pack4(ws)
    return {"h": bf(h), "w1_words": w1_words, "w1_scales": w1_scales, "tb": bf(tb), "g": bf(g), "e": bf(e), "ws_words": ws_words, "ws_scales": ws_scales, "c": bf(c)}


def core(h, w1_words, w1_scales, tb, g, e, ws_words, ws_scales, c):
    k = mxq(f64(h), 2, "e4m3") @ unpack4(w1_words, w1_scales)
    l = 2.0 * np.tanh(k) + f64(tb)[:, :, None]
    p = stable_softmax(l, 1)
    a = np.sqrt(S) * p * f64(g)[:, :, None]
    u = mxq(f64(e), 2, "e4m3") @ unpack4(ws_words, ws_scales)
    v = mxq(a, 1, "e4m3").transpose(0, 2, 1) @ mxq(u, 1, "e4m3")
    q = np.sum(v * f64(c)[:, None, :], axis=-1) / np.sqrt(D)
    alpha = stable_softmax(q, 1)
    return M * alpha[:, :, None] * v


def reference(h, w1_words, w1_scales, tb, g, e, ws_words, ws_scales, c):
    R_out = core(h, w1_words, w1_scales, tb, g, e, ws_words, ws_scales, c)
    words, scales = planes(np.moveaxis(R_out, 2, 0).reshape(512, -1))
    return R_out, words, scales

@@ -1,0 +1,270 @@
+import math
+from contextlib import ExitStack
+
+import concourse.mybir as mybir
+from concourse.masks import make_identity
+
+B, S, D, M = 8, 512, 512, 256
+P = 128
+FLOPS = 2 * B * (S * D * M + S * D * D + M * S * D)
+
+F32 = mybir.dt.float32
+BF16 = mybir.dt.bfloat16
+I32 = mybir.dt.int32
+U32 = mybir.dt.uint32
+U8 = mybir.dt.uint8
+FP8X4 = mybir.dt.float8_e4m3fn_x4
+FP4X4 = mybir.dt.float4_e2m1fn_x4
+AF = mybir.ActivationFunctionType
+ALU = mybir.AluOpType
+AX = mybir.AxisListType
+
+STEPS = [("O1", 6), ("Xe0", 1), ("O0", 6), ("U1", 3), ("Z", 3), ("Y0", 4), ("V0", 5), ("A1", 4), ("V1", 5), ("D0", 5), ("D1", 5), ("U3", 3), ("Y1", 3), ("K0", 1), ("E", 2), ("Th0", 0), ("P0", 8), ("Y3", 3), ("H0", 1), ("RZ", 3), ("Qu", 4), ("Th1", 0), ("QR", 5), ("U2", 2), ("Xh0", 0), ("MN", 5), ("Xh1", 0), ("Y2", 2), ("G", 2), ("K1", 1), ("ER", 5), ("R1", 7), ("Qp", 10), ("P1", 8), ("ZR", 3), ("Qe", 1), ("Te1", 0), ("H1", 1), ("EO", 5), ("RS", 5), ("Te0", 0), ("W", 8), ("Qa", 4), ("Xe1", 0), ("AL", 5), ("Qh", 0), ("R0", 6), ("A0", 3), ("U0", 3)]
+ENGINE = {"Xh0": "V", "Xh1": "S", "Xe0": "V", "Xe1": "S", "Y0": "S", "Y1": "S", "Y2": "S", "Y3": "S", "O0": "S", "O1": "S", "W": "S"}
+
+
+def tile_comireclabelawareinterests_x2_kernel(tc, h, w1_words, w1_scales, tb, g, e, ws_words, ws_scales, c, out_0, out_1, out_2):
+    nc = tc.nc
+    with ExitStack() as ctx:
+        keep = ctx.enter_context(tc.tile_pool(name="keep", bufs=1))
+        work = ctx.enter_context(tc.tile_pool(name="work", bufs=3))
+        small = ctx.enter_context(tc.tile_pool(name="small", bufs=4))
+        pools = {
+            "bank": (ctx.enter_context(tc.psum_pool(name="ps_t", bufs=2)), 512),
+            "kb": (ctx.enter_context(tc.psum_pool(name="ps_k", bufs=2)), 512),
+            "v": (ctx.enter_context(tc.psum_pool(name="ps_v", bufs=2)), 512),
+            "sm": (ctx.enter_context(tc.psum_pool(name="ps_s", bufs=2)), 512),
+        }
+
+        w1w = keep.tile([P, 2 * M], U8, name="w1w", align_bytes=64)
+        w1s = keep.tile([P, M], U8, name="w1s", align_bytes=64)
+        wsw = keep.tile([P, 2 * D], U8, name="wsw", align_bytes=64)
+        wss = keep.tile([P, D], U8, name="wss", align_bytes=64)
+        tb_sb = keep.tile([P, S], BF16, name="tb_sb")
+        g_sb = keep.tile([P, S], BF16, name="g_sb")
+        wg = keep.tile([P, S], F32, name="wg")
+        cb = keep.tile([P, B, D], BF16, name="cb")
+        wcol = keep.tile([P, 4, 40], F32, name="wcol")
+        ident = keep.tile([P, P], F32, name="ident")
+        pscale = keep.tile([P, B * M], U8, name="pscale", align_bytes=64)
+
+        SPEC = {
+            "h": ([P, 4, D], BF16, 6), "e": ([P, 4, D], BF16, 6),
+            "hg": ([P, S, 4], BF16, 3), "eg": ([P, S, 4], BF16, 3),
+            "hc": ([P, S], U32, 3), "ec": ([P, S], U32, 3), "hs": ([P, S], U8, 3), "es": ([P, S], U8, 3),
+            "tanh": ([P, 4, M], F32, 3), "ex": ([P, 4, M], F32, 3), "exg": ([P, 4, M], F32, 3),
+            "ag": ([P, M, 4], BF16, 3), "ac": ([P, M], U32, 4), "as": ([P, M], U8, 4),
+            "ug": ([P, D, 4], BF16, 3), "uc": ([P, D], U32, 4), "us": ([P, D], U8, 4),
+            "junk": ([P, D], F32, 2), "o": ([P, 2, D], F32, 4), "ob": ([P, 2, D], BF16, 9),
+            "pg": ([P, M, 4], BF16, 3), "pc": ([P, M], U32, 4), "erow": ([P, M], F32, 2),
+            "rz": ([P, 2], F32, 4), "qn": ([P, 2], F32, 4), "mn": ([P, 1], F32, 4), "esum": ([P, 1], F32, 4),
+            "eown": ([P, 2], F32, 4), "rs": ([P, 1], F32, 4), "alpha": ([P, 2], F32, 4),
+        }
+        made = {}
+
+        def buf(name, b):
+            if (name, b) not in made:
+                shape, dtype, bufs = SPEC[name]
+                t = work.tile(shape, dtype, name=name, bufs=bufs, align_bytes=64)
+                made[name, b] = t
+            return made[name, b]
+
+        def bank(pool, name, b):
+            t = pools[pool][0].tile([P, 512], F32, name=pool)
+            made[name, b] = t
+            return t
+
+        def load(name, src, b):
+            t = buf(name, b)
+            v = src[b].rearrange("(p t) f -> p t f", t=4)
+            if b == 0:
+                nc.sync.dma_start(out=t[:, 0:2, :], in_=v[:, 0:2, :])
+                nc.sync.dma_start(out=t[:, 2:4, :], in_=v[:, 2:4, :])
+            else:
+                nc.sync.dma_start(out=t[:], in_=v)
+
+        def evac(step, dst, src):
+            if ENGINE[step] == "V":
+                nc.vector.tensor_copy(out=dst, in_=src)
+            else:
+                nc.scalar.copy(out=dst, in_=src)
+
+        def words_of(t):
+            return t[:].rearrange("p a k -> p (a k)").bitcast(F32)
+
+        def col(t, i, n=P):
+            return t[:, n * i:n * i + n]
+
+        def token_weights():
+            mx = small.tile([P, 1], F32, name="mx")
+            nc.vector.tensor_reduce(out=mx[0:40, :], in_=tb_sb[0:40, :], axis=AX.X, op=ALU.max)
+            nb = small.tile([P, 1], F32, name="nb")
+            nc.vector.tensor_scalar(out=nb[0:40, :], in0=mx[0:40, :], scalar1=-1.0, scalar2=-2.0, op0=ALU.mult, op1=ALU.add)
+            nc.scalar.activation(out=wg[0:40, :], in_=tb_sb[0:40, :], func=AF.Exp, bias=nb[0:40, :])
+            nc.vector.scalar_tensor_tensor(out=wg[32:40, :], in0=g_sb[32:40, :], scalar=math.sqrt(S), in1=wg[32:40, :], op0=ALU.mult, op1=ALU.mult)
+            wbank = bank("bank", "wbank", 0)
+            for t in range(4):
+                nc.tensor.transpose(col(wbank, t), wg[:, t:t + 509:4], ident[:])
+            nc.vector.tensor_copy(out=wcol[:], in_=wbank[:].rearrange("p (t n) -> p t n", t=4)[:, :, 0:40])
+
+        def turn(x, half, b):
+            t = bank("bank", "T%s%d" % (x, half), b)
+            words = words_of(buf(x, b))
+            for tt in range(2):
+                for u in range(2):
+                    w0 = 256 * (2 * half + tt) + u
+                    nc.tensor.transpose(col(t, 2 * tt + u), words[:, w0:w0 + 255:2], ident[:])
+
+        def unload(x, half, b):
+            dst = words_of(buf(x + "g", b)).rearrange("p (s u) -> p s u", u=2)[:, 256 * half:256 * half + 256, :]
+            evac("X%s%d" % (x, half), dst.rearrange("p (t r) u -> p t r u", t=2), made["T%s%d" % (x, half), b][:].rearrange("p (t u r) -> p t r u", t=2, u=2))
+
+        def quantize(codes, scales, src):
+            nc.vector.quantize_mx(out=codes.bitcast(FP8X4), scales=scales, in_=src[:].rearrange("p a k -> p (a k)"))
+
+        def mm_k(half, b):
+            t = bank("kb", "K%d" % half, b)
+            for tt in range(2):
+                cols = slice(P * (2 * half + tt), P * (2 * half + tt + 1))
+                nc.tensor.matmul_mx(out=col(t, tt, M), lhsT=buf("hc", b)[:, cols].bitcast(FP8X4), lhsT_scale=buf("hs", b)[:, cols], rhs=w1w[:].bitcast(FP4X4), rhs_scale=w1s[:], start=True, stop=True)
+
+        def tanh(half, b):
+            nc.scalar.activation(out=buf("tanh", b)[:, 2 * half:2 * half + 2, :], in_=made["K%d" % half, b][:].rearrange("p (t m) -> p t m", t=2), func=AF.Tanh)
+
+        def expo(b):
+            if b == 0:
+                token_weights()
+            nc.scalar.activation(out=buf("ex", b)[:], in_=buf("tanh", b)[:], func=AF.Exp, scale=2.0)
+
+        def gain(b):
+            for t in range(4):
+                nc.vector.tensor_scalar(out=buf("exg", b)[:, t, :], in0=buf("ex", b)[:, t, :], scalar1=wcol[:, t, 32 + b:33 + b], scalar2=None, op0=ALU.mult)
+
+        def zsum(b):
+            zt = bank("sm", "Z", b)
+            for i in range(2):
+                for t in range(4):
+                    nc.tensor.matmul(zt[:, i:i + 1], lhsT=buf("ex", b)[:, t, P * i:P * i + P], rhs=wcol[:, t, b:b + 1], start=(t == 0), stop=(t == 3))
+
+        def zrec(b):
+            nc.vector.reciprocal(out=buf("rz", b)[:], in_=made["Z", b][:, 0:2])
+
+        def zrow(b):
+            for i in range(2):
+                nc.tensor.transpose(col(made["Z", b], 2 + i), buf("rz", b)[:, i:i + 1].to_broadcast([P, P]), ident[:])
+
+        def amul(i, b):
+            ms = slice(P * i, P * i + P)
+            nc.vector.tensor_tensor(out=buf("ag", b)[:, ms, :], in0=buf("exg", b)[:, :, ms].rearrange("p t m -> p m t"), in1=col(made["Z", b], 2 + i).unsqueeze(2).to_broadcast([P, P, 4]), op=ALU.mult)
+
+        def mm_u(q, b):
+            t = bank("kb", "U%d" % q, b)
+            for tt in range(4):
+                nc.tensor.matmul_mx(out=col(t, tt), lhsT=col(buf("ec", b), tt).bitcast(FP8X4), lhsT_scale=col(buf("es", b), tt), rhs=wsw[:, 256 * q:256 * q + 256].bitcast(FP4X4), rhs_scale=col(wss, q), start=True, stop=True)
+
+        def uout(q, b):
+            evac("Y%d" % q, buf("ug", b)[:, P * q:P * q + P, :], made["U%d" % q, b][:].rearrange("p (t j) -> p j t", t=4))
+
+        def mm_v(i, b):
+            v = bank("v", "V%d" % i, b)
+            nc.tensor.matmul_mx(out=v[:], lhsT=col(buf("ac", b), i).bitcast(FP8X4), lhsT_scale=col(buf("as", b), i), rhs=buf("uc", b)[:].bitcast(FP8X4), rhs_scale=buf("us", b)[:], start=True, stop=True)
+
+        def qdot(i, b):
+            junk = work.tile([P, D], F32, name="junk", bufs=2, align_bytes=64)
+            nc.vector.scalar_tensor_tensor(out=junk[:], in0=made["V%d" % i, b][:], scalar=-1.0 / math.sqrt(D), in1=cb[:, b, :], op0=ALU.mult, op1=ALU.mult, accum_out=buf("qn", b)[:, i:i + 1])
+
+        def qrow(b):
+            t = bank("sm", "Q", b)
+            for i in range(2):
+                nc.tensor.transpose(col(t, i), buf("qn", b)[:, i:i + 1].to_broadcast([P, P]), ident[:])
+
+        def qmin(b):
+            nc.vector.tensor_reduce(out=buf("mn", b)[:], in_=made["Q", b][:, 0:M], axis=AX.X, op=ALU.min)
+
+        def erow(b):
+            nc.scalar.activation(out=buf("erow", b)[:], in_=made["Q", b][:, 0:M], func=AF.Exp, scale=-1.0, bias=buf("mn", b)[:], accum_out=buf("esum", b)[:])
+
+        def eown(b):
+            nc.scalar.activation(out=buf("eown", b)[:], in_=buf("qn", b)[:], func=AF.Exp, scale=-1.0, bias=buf("mn", b)[:])
+
+        def rsum(b):
+            nc.vector.reciprocal(out=buf("rs", b)[:], in_=buf("esum", b)[:])
+
+        def alpha(b):
+            nc.vector.tensor_scalar(out=buf("alpha", b)[:], in0=buf("eown", b)[:], scalar1=buf("rs", b)[:], scalar2=float(M), op0=ALU.mult, op1=ALU.mult)
+
+        def outp(i, b):
+            o = buf("o", b)
+            if ENGINE["O%d" % i] == "V":
+                nc.vector.tensor_scalar(out=o[:, i, :], in0=made["V%d" % i, b][:], scalar1=buf("alpha", b)[:, i:i + 1], scalar2=None, op0=ALU.mult)
+            else:
+                nc.scalar.activation(out=o[:, i, :], in_=made["V%d" % i, b][:], func=AF.Copy, scale=buf("alpha", b)[:, i:i + 1])
+            nc.sync.dma_start(out=out_0[b, P * i:P * i + P, :], in_=o[:, i, :])
+
+        def rnd(i, b):
+            nc.vector.tensor_copy(out=buf("ob", b)[:, i, :], in_=buf("o", b)[:, i, :])
+
+        def pturn(i, b):
+            if i == 0:
+                bank("bank", "P", b)
+            for u in range(2):
+                nc.tensor.transpose(col(made["P", b], 2 * i + u), buf("ob", b)[:, i, :].bitcast(F32)[:, u:u + 255:2], ident[:])
+
+        def pout(b):
+            evac("W", words_of(buf("pg", b)).rearrange("p (i m u) -> p i m u", i=2, u=2), made["P", b][:].rearrange("p (i u m) -> p i m u", i=2, u=2))
+
+        def pquant(b):
+            quantize(buf("pc", b)[:], col(pscale, b, M), buf("pg", b))
+            nc.sync.dma_start(out=out_1[0, :, M * b:M * b + M, :].rearrange("p m t -> p (m t)").bitcast(I32), in_=buf("pc", b)[:].bitcast(I32))
+            if b == B - 1:
+                for q in range(4):
+                    nc.sync.dma_start(out=out_2[0, 4 * q:4 * q + 4, :].bitcast(I32), in_=pscale[32 * q:32 * q + 4, :].bitcast(I32))
+
+        DO = {
+            "Qh": lambda b: quantize(buf("hc", b)[:], buf("hs", b)[:], buf("hg", b)),
+            "Qe": lambda b: quantize(buf("ec", b)[:], buf("es", b)[:], buf("eg", b)),
+            "Qa": lambda b: quantize(buf("ac", b)[:], buf("as", b)[:], buf("ag", b)),
+            "Qu": lambda b: quantize(buf("uc", b)[:], buf("us", b)[:], buf("ug", b)),
+            "E": expo, "G": gain, "Z": zsum, "RZ": zrec, "ZR": zrow, "QR": qrow, "MN": qmin, "ER": erow, "EO": eown,
+            "RS": rsum, "AL": alpha, "W": pout, "Qp": pquant,
+        }
+        for i in range(2):
+            for x in "he":
+                DO["T%s%d" % (x, i)] = lambda b, x=x, i=i: turn(x, i, b)
+                DO["X%s%d" % (x, i)] = lambda b, x=x, i=i: unload(x, i, b)
+            for name, fn in (("K", mm_k), ("H", tanh), ("A", amul), ("V", mm_v), ("D", qdot), ("O", outp), ("R", rnd), ("P", pturn)):
+                DO["%s%d" % (name, i)] = lambda b, fn=fn, i=i: fn(i, b)
+        for q in range(4):
+            DO["U%d" % q] = lambda b, q=q: mm_u(q, b)
+            DO["Y%d" % q] = lambda b, q=q: uout(q, b)
+
+        with tc.manual_schedule():
+            load("h", h, 0)
+            nc.vector.memset(w1s[:].bitcast(I32), 0)
+            nc.vector.memset(wss[:].bitcast(I32), 0)
+            nc.vector.memset(tb_sb[:], 0.0)
+            make_identity(nc, ident[:])
+            nc.vector.memset(wg[:], 0.0)
+            nc.gpsimd.dma_start(out=tb_sb[0:8, :], in_=tb[:, :])
+            nc.gpsimd.dma_start(out=tb_sb[32:40, :], in_=tb[:, :])
+            nc.gpsimd.dma_start(out=g_sb[32:40, :], in_=g[:, :])
+            for q in range(4):
+                nc.gpsimd.dma_start(out=wss[32 * q:32 * q + 4, :].bitcast(I32), in_=ws_scales[0, 4 * q:4 * q + 4, :].bitcast(I32))
+            nc.sync.dma_start(out=w1w[:].bitcast(I32), in_=w1_words[0].bitcast(I32))
+            for q in range(4):
+                nc.sync.dma_start(out=w1s[32 * q:32 * q + 4, :].bitcast(I32), in_=w1_scales[0, 4 * q:4 * q + 4, :].bitcast(I32))
+            load("e", e, 0)
+            nc.sync.dma_start(out=wsw[:].bitcast(I32), in_=ws_words[0].bitcast(I32))
+            load("h", h, 1)
+            load("e", e, 1)
+            load("h", h, 2)
+            load("e", e, 2)
+            nc.sync.dma_start(out=cb[:].rearrange("p b j -> p (b j)"), in_=c.rearrange("b j -> (b j)").partition_broadcast(P))
+            last = max(lag for step, lag in STEPS)
+            for n in range(B + last):
+                if 3 <= n + 3 < B:
+                    load("h", h, n + 3)
+                    load("e", e, n + 3)
+                for step, lag in STEPS:
+                    if 0 <= n - lag < B:
+                        DO[step](n - lag)

@@ -19,8 +19,8 @@ AF = mybir.ActivationFunctionType
 ALU = mybir.AluOpType
 AX = mybir.AxisListType
 
-STEPS = [("O1", 6), ("Xe0", 1), ("O0", 6), ("U1", 3), ("Z", 3), ("Y0", 4), ("V0", 5), ("A1", 4), ("V1", 5), ("D0", 5), ("D1", 5), ("U3", 3), ("Y1", 3), ("K0", 1), ("E", 2), ("Th0", 0), ("P0", 8), ("Y3", 3), ("H0", 1), ("RZ", 3), ("Qu", 4), ("Th1", 0), ("QR", 5), ("U2", 2), ("Xh0", 0), ("MN", 5), ("Xh1", 0), ("Y2", 2), ("G", 2), ("K1", 1), ("ER", 5), ("R1", 7), ("Qp", 10), ("P1", 8), ("ZR", 3), ("Qe", 1), ("Te1", 0), ("H1", 1), ("EO", 5), ("RS", 5), ("Te0", 0), ("W", 8), ("Qa", 4), ("Xe1", 0), ("AL", 5), ("Qh", 0), ("R0", 6), ("A0", 3), ("U0", 3)]
-ENGINE = {"Xh0": "V", "Xh1": "S", "Xe0": "V", "Xe1": "S", "Y0": "S", "Y1": "S", "Y2": "S", "Y3": "S", "O0": "S", "O1": "S", "W": "S"}
+STEPS = [("A0", 4), ("Y3", 4), ("Xh1", 1), ("V0", 5), ("A1", 4), ("E", 2), ("Qh", 1), ("V1", 5), ("U1", 3), ("RZ", 3), ("U0", 3), ("Te0", 1), ("Y1", 3), ("D0", 5), ("D1", 5), ("Te1", 1), ("QR", 5), ("G", 3), ("Xe0", 1), ("R0", 7), ("Y0", 3), ("K0", 1), ("K1", 1), ("ZR", 3), ("Th0", 0), ("MN", 5), ("Xe1", 1), ("H0", 1), ("P0", 8), ("ER", 5), ("H1", 1), ("Qu", 4), ("P1", 8), ("EO", 5), ("Th1", 0), ("Qe", 1), ("W", 8), ("RS", 5), ("Qa", 4), ("AL", 5), ("Xh0", 0), ("U2", 3), ("U3", 3), ("Z", 2), ("O1", 5), ("O0", 5), ("Y2", 3), ("R1", 7), ("Qp", 10)]
+ENGINE = {"Xh0": "S", "Xh1": "V", "Xe0": "V", "Xe1": "S", "Y0": "S", "Y1": "S", "Y2": "S", "Y3": "S", "O0": "S", "O1": "S", "W": "S"}
 
 
 def tile_comireclabelawareinterests_x2_kernel(tc, h, w1_words, w1_scales, tb, g, e, ws_words, ws_scales, c, out_0, out_1, out_2):
@@ -42,9 +42,9 @@ def tile_comireclabelawareinterests_x2_kernel(tc, h, w1_words, w1_scales, tb, g,
         wss = keep.tile([P, D], U8, name="wss", align_bytes=64)
         tb_sb = keep.tile([P, S], BF16, name="tb_sb")
         g_sb = keep.tile([P, S], BF16, name="g_sb")
-        wg = keep.tile([P, S], F32, name="wg")
+        wg = keep.tile([P, 2, S], F32, name="wg")
         cb = keep.tile([P, B, D], BF16, name="cb")
-        wcol = keep.tile([P, 4, 40], F32, name="wcol")
+        wcol = keep.tile([P, 4, 2 * B], F32, name="wcol")
         ident = keep.tile([P, P], F32, name="ident")
         pscale = keep.tile([P, B * M], U8, name="pscale", align_bytes=64)
 
@@ -97,15 +97,16 @@ def tile_comireclabelawareinterests_x2_kernel(tc, h, w1_words, w1_scales, tb, g,
 
         def token_weights():
             mx = small.tile([P, 1], F32, name="mx")
-            nc.vector.tensor_reduce(out=mx[0:40, :], in_=tb_sb[0:40, :], axis=AX.X, op=ALU.max)
+            nc.vector.tensor_reduce(out=mx[0:8, :], in_=tb_sb[0:8, :], axis=AX.X, op=ALU.max)
             nb = small.tile([P, 1], F32, name="nb")
-            nc.vector.tensor_scalar(out=nb[0:40, :], in0=mx[0:40, :], scalar1=-1.0, scalar2=-2.0, op0=ALU.mult, op1=ALU.add)
-            nc.scalar.activation(out=wg[0:40, :], in_=tb_sb[0:40, :], func=AF.Exp, bias=nb[0:40, :])
-            nc.vector.scalar_tensor_tensor(out=wg[32:40, :], in0=g_sb[32:40, :], scalar=math.sqrt(S), in1=wg[32:40, :], op0=ALU.mult, op1=ALU.mult)
-            wbank = bank("bank", "wbank", 0)
-            for t in range(4):
-                nc.tensor.transpose(col(wbank, t), wg[:, t:t + 509:4], ident[:])
-            nc.vector.tensor_copy(out=wcol[:], in_=wbank[:].rearrange("p (t n) -> p t n", t=4)[:, :, 0:40])
+            nc.vector.tensor_scalar(out=nb[0:8, :], in0=mx[0:8, :], scalar1=-1.0, scalar2=-2.0, op0=ALU.mult, op1=ALU.add)
+            nc.scalar.activation(out=wg[0:8, 0, :], in_=tb_sb[0:8, :], func=AF.Exp, bias=nb[0:8, :])
+            nc.vector.scalar_tensor_tensor(out=wg[0:8, 1, :], in0=g_sb[0:8, :], scalar=math.sqrt(S), in1=wg[0:8, 0, :], op0=ALU.mult, op1=ALU.mult)
+            for r in range(2):
+                wbank = bank("bank", "wbank", r)
+                for t in range(4):
+                    nc.tensor.transpose(col(wbank, t), wg[:, r, t:t + 509:4], ident[:])
+                nc.vector.tensor_copy(out=wcol[:, :, B * r:B * r + B], in_=wbank[:].rearrange("p (t n) -> p t n", t=4)[:, :, 0:B])
 
         def turn(x, half, b):
             t = bank("bank", "T%s%d" % (x, half), b)
@@ -138,7 +139,7 @@ def tile_comireclabelawareinterests_x2_kernel(tc, h, w1_words, w1_scales, tb, g,
 
         def gain(b):
             for t in range(4):
-                nc.vector.tensor_scalar(out=buf("exg", b)[:, t, :], in0=buf("ex", b)[:, t, :], scalar1=wcol[:, t, 32 + b:33 + b], scalar2=None, op0=ALU.mult)
+                nc.vector.tensor_scalar(out=buf("exg", b)[:, t, :], in0=buf("ex", b)[:, t, :], scalar1=wcol[:, t, B + b:B + b + 1], scalar2=None, op0=ALU.mult)
 
         def zsum(b):
             zt = bank("sm", "Z", b)
@@ -242,20 +243,18 @@ def tile_comireclabelawareinterests_x2_kernel(tc, h, w1_words, w1_scales, tb, g,
             load("h", h, 0)
             nc.vector.memset(w1s[:].bitcast(I32), 0)
             nc.vector.memset(wss[:].bitcast(I32), 0)
-            nc.vector.memset(tb_sb[:], 0.0)
+            nc.gpsimd.memset(wg[:], 0.0)
             make_identity(nc, ident[:])
-            nc.vector.memset(wg[:], 0.0)
-            nc.gpsimd.dma_start(out=tb_sb[0:8, :], in_=tb[:, :])
-            nc.gpsimd.dma_start(out=tb_sb[32:40, :], in_=tb[:, :])
-            nc.gpsimd.dma_start(out=g_sb[32:40, :], in_=g[:, :])
-            for q in range(4):
-                nc.gpsimd.dma_start(out=wss[32 * q:32 * q + 4, :].bitcast(I32), in_=ws_scales[0, 4 * q:4 * q + 4, :].bitcast(I32))
             nc.sync.dma_start(out=w1w[:].bitcast(I32), in_=w1_words[0].bitcast(I32))
             for q in range(4):
                 nc.sync.dma_start(out=w1s[32 * q:32 * q + 4, :].bitcast(I32), in_=w1_scales[0, 4 * q:4 * q + 4, :].bitcast(I32))
             load("e", e, 0)
             nc.sync.dma_start(out=wsw[:].bitcast(I32), in_=ws_words[0].bitcast(I32))
             load("h", h, 1)
+            nc.sync.dma_start(out=tb_sb[0:8, :], in_=tb[:, :])
+            nc.sync.dma_start(out=g_sb[0:8, :], in_=g[:, :])
+            for q in range(4):
+                nc.sync.dma_start(out=wss[32 * q:32 * q + 4, :].bitcast(I32), in_=ws_scales[0, 4 * q:4 * q + 4, :].bitcast(I32))
             load("e", e, 1)
             load("h", h, 2)
             load("e", e, 2)

@@ -19,8 +19,8 @@ AF = mybir.ActivationFunctionType
 ALU = mybir.AluOpType
 AX = mybir.AxisListType
 
-STEPS = [("A0", 4), ("Y3", 4), ("Xh1", 1), ("V0", 5), ("A1", 4), ("E", 2), ("Qh", 1), ("V1", 5), ("U1", 3), ("RZ", 3), ("U0", 3), ("Te0", 1), ("Y1", 3), ("D0", 5), ("D1", 5), ("Te1", 1), ("QR", 5), ("G", 3), ("Xe0", 1), ("R0", 7), ("Y0", 3), ("K0", 1), ("K1", 1), ("ZR", 3), ("Th0", 0), ("MN", 5), ("Xe1", 1), ("H0", 1), ("P0", 8), ("ER", 5), ("H1", 1), ("Qu", 4), ("P1", 8), ("EO", 5), ("Th1", 0), ("Qe", 1), ("W", 8), ("RS", 5), ("Qa", 4), ("AL", 5), ("Xh0", 0), ("U2", 3), ("U3", 3), ("Z", 2), ("O1", 5), ("O0", 5), ("Y2", 3), ("R1", 7), ("Qp", 10)]
-ENGINE = {"Xh0": "S", "Xh1": "V", "Xe0": "V", "Xe1": "S", "Y0": "S", "Y1": "S", "Y2": "S", "Y3": "S", "O0": "S", "O1": "S", "W": "S"}
+STEPS = [("Xe1", 1), ("ZR", 2), ("D1", 3), ("D0", 3), ("Th0", 0), ("H0", 1), ("A0", 2), ("H1", 1), ("Xh0", 0), ("Th1", 0), ("A1", 2), ("U1", 2), ("U0", 2), ("E", 1), ("C0", 4), ("Y1", 2), ("Y0", 2), ("Xh1", 0), ("QR", 3), ("Te0", 1), ("MN", 3), ("Qp", 4), ("U3", 2), ("ER", 3), ("U2", 2), ("Te1", 0), ("G", 1), ("RS", 3), ("EO", 3), ("Qh", 0), ("Y3", 2), ("AR", 3), ("Qa", 2), ("Y2", 2), ("AL", 3), ("B1", 3), ("Xe0", 1), ("Qu", 2), ("O1", 3), ("Z", 1), ("K0", 0), ("C1", 3), ("Qe", 1), ("B0", 3), ("V1", 2), ("O0", 3), ("K1", 0), ("V0", 2), ("RZ", 1)]
+ENGINE = {"Xh0": "S", "Xh1": "V", "Xe0": "S", "Xe1": "S", "Y0": "S", "Y1": "S", "Y2": "S", "Y3": "S", "O0": "S", "O1": "S"}
 
 
 def tile_comireclabelawareinterests_x2_kernel(tc, h, w1_words, w1_scales, tb, g, e, ws_words, ws_scales, c, out_0, out_1, out_2):
@@ -31,15 +31,17 @@ def tile_comireclabelawareinterests_x2_kernel(tc, h, w1_words, w1_scales, tb, g,
         small = ctx.enter_context(tc.tile_pool(name="small", bufs=4))
         pools = {
             "bank": (ctx.enter_context(tc.psum_pool(name="ps_t", bufs=2)), 512),
-            "kb": (ctx.enter_context(tc.psum_pool(name="ps_k", bufs=2)), 512),
+            "kb": (ctx.enter_context(tc.psum_pool(name="ps_k", bufs=3)), 512),
             "v": (ctx.enter_context(tc.psum_pool(name="ps_v", bufs=2)), 512),
-            "sm": (ctx.enter_context(tc.psum_pool(name="ps_s", bufs=2)), 512),
+            "sm": (ctx.enter_context(tc.psum_pool(name="ps_s", bufs=1)), 512),
         }
 
         w1w = keep.tile([P, 2 * M], U8, name="w1w", align_bytes=64)
         w1s = keep.tile([P, M], U8, name="w1s", align_bytes=64)
         wsw = keep.tile([P, 2 * D], U8, name="wsw", align_bytes=64)
         wss = keep.tile([P, D], U8, name="wss", align_bytes=64)
+        wsw_in = keep.tile([P, 2 * D], U8, name="wsw_in", align_bytes=64)
+        wss_in = keep.tile([P, D], U8, name="wss_in", align_bytes=64)
         tb_sb = keep.tile([P, S], BF16, name="tb_sb")
         g_sb = keep.tile([P, S], BF16, name="g_sb")
         wg = keep.tile([P, 2, S], F32, name="wg")
@@ -55,8 +57,7 @@ def tile_comireclabelawareinterests_x2_kernel(tc, h, w1_words, w1_scales, tb, g,
             "tanh": ([P, 4, M], F32, 3), "ex": ([P, 4, M], F32, 3), "exg": ([P, 4, M], F32, 3),
             "ag": ([P, M, 4], BF16, 3), "ac": ([P, M], U32, 4), "as": ([P, M], U8, 4),
             "ug": ([P, D, 4], BF16, 3), "uc": ([P, D], U32, 4), "us": ([P, D], U8, 4),
-            "junk": ([P, D], F32, 2), "o": ([P, 2, D], F32, 4), "ob": ([P, 2, D], BF16, 9),
-            "pg": ([P, M, 4], BF16, 3), "pc": ([P, M], U32, 4), "erow": ([P, M], F32, 2),
+            "junk": ([P, D], F32, 2), "o": ([P, 2, D], F32, 4), "pg": ([P, M, 4], BF16, 3), "pc": ([P, M], U32, 4), "erow": ([P, M], F32, 3), "arow": ([P, M], F32, 3),
             "rz": ([P, 2], F32, 4), "qn": ([P, 2], F32, 4), "mn": ([P, 1], F32, 4), "esum": ([P, 1], F32, 4),
             "eown": ([P, 2], F32, 4), "rs": ([P, 1], F32, 4), "alpha": ([P, 2], F32, 4),
         }
@@ -108,6 +109,10 @@ def tile_comireclabelawareinterests_x2_kernel(tc, h, w1_words, w1_scales, tb, g,
                     nc.tensor.transpose(col(wbank, t), wg[:, r, t:t + 509:4], ident[:])
                 nc.vector.tensor_copy(out=wcol[:, :, B * r:B * r + B], in_=wbank[:].rearrange("p (t n) -> p t n", t=4)[:, :, 0:B])
 
+        def permute_ws():
+            nc.vector.tensor_copy(out=wss[:].rearrange("p (t m) -> p m t", t=4), in_=wss_in[:].rearrange("p (m t) -> p m t", t=4))
+            nc.vector.tensor_copy(out=wsw[:].rearrange("p (t m b) -> p m t b", t=4, b=2), in_=wsw_in[:].rearrange("p (m t b) -> p m t b", t=4, b=2))
+
         def turn(x, half, b):
             t = bank("bank", "T%s%d" % (x, half), b)
             words = words_of(buf(x, b))
@@ -145,10 +150,10 @@ def tile_comireclabelawareinterests_x2_kernel(tc, h, w1_words, w1_scales, tb, g,
             zt = bank("sm", "Z", b)
             for i in range(2):
                 for t in range(4):
-                    nc.tensor.matmul(zt[:, i:i + 1], lhsT=buf("ex", b)[:, t, P * i:P * i + P], rhs=wcol[:, t, b:b + 1], start=(t == 0), stop=(t == 3))
+                    nc.tensor.matmul(zt[:, 64 * i:64 * i + 64], lhsT=buf("ex", b)[:, t, P * i:P * i + P], rhs=wcol[:, t, b:b + 1].to_broadcast([P, 64]), start=(t == 0), stop=(t == 3))
 
         def zrec(b):
-            nc.vector.reciprocal(out=buf("rz", b)[:], in_=made["Z", b][:, 0:2])
+            nc.vector.reciprocal(out=buf("rz", b)[:], in_=made["Z", b][:, 0:65:64])
 
         def zrow(b):
             for i in range(2):
@@ -172,7 +177,7 @@ def tile_comireclabelawareinterests_x2_kernel(tc, h, w1_words, w1_scales, tb, g,
 
         def qdot(i, b):
             junk = work.tile([P, D], F32, name="junk", bufs=2, align_bytes=64)
-            nc.vector.scalar_tensor_tensor(out=junk[:], in0=made["V%d" % i, b][:], scalar=-1.0 / math.sqrt(D), in1=cb[:, b, :], op0=ALU.mult, op1=ALU.mult, accum_out=buf("qn", b)[:, i:i + 1])
+            nc.vector.scalar_tensor_tensor(out=junk[:].rearrange("p (m t) -> p m t", t=4), in0=made["V%d" % i, b][:].rearrange("p (t m) -> p m t", t=4), scalar=-1.0 / math.sqrt(D), in1=cb[:, b, :].rearrange("p (m t) -> p m t", t=4), op0=ALU.mult, op1=ALU.mult, accum_out=buf("qn", b)[:, i:i + 1])
 
         def qrow(b):
             t = bank("sm", "Q", b)
@@ -197,22 +202,21 @@ def tile_comireclabelawareinterests_x2_kernel(tc, h, w1_words, w1_scales, tb, g,
         def outp(i, b):
             o = buf("o", b)
             if ENGINE["O%d" % i] == "V":
-                nc.vector.tensor_scalar(out=o[:, i, :], in0=made["V%d" % i, b][:], scalar1=buf("alpha", b)[:, i:i + 1], scalar2=None, op0=ALU.mult)
+                nc.vector.tensor_scalar(out=o[:, i, :].rearrange("p (m t) -> p m t", t=4), in0=made["V%d" % i, b][:].rearrange("p (t m) -> p m t", t=4), scalar1=buf("alpha", b)[:, i:i + 1], scalar2=None, op0=ALU.mult)
             else:
-                nc.scalar.activation(out=o[:, i, :], in_=made["V%d" % i, b][:], func=AF.Copy, scale=buf("alpha", b)[:, i:i + 1])
+                nc.scalar.activation(out=o[:, i, :].rearrange("p (m t) -> p m t", t=4), in_=made["V%d" % i, b][:].rearrange("p (t m) -> p m t", t=4), func=AF.Copy, scale=buf("alpha", b)[:, i:i + 1])
             nc.sync.dma_start(out=out_0[b, P * i:P * i + P, :], in_=o[:, i, :])
 
-        def rnd(i, b):
-            nc.vector.tensor_copy(out=buf("ob", b)[:, i, :], in_=buf("o", b)[:, i, :])
+        def arow(b):
+            nc.vector.tensor_scalar(out=buf("arow", b)[:], in0=buf("erow", b)[:], scalar1=buf("rs", b)[:], scalar2=float(M), op0=ALU.mult, op1=ALU.mult)
 
-        def pturn(i, b):
-            if i == 0:
-                bank("bank", "P", b)
-            for u in range(2):
-                nc.tensor.transpose(col(made["P", b], 2 * i + u), buf("ob", b)[:, i, :].bitcast(F32)[:, u:u + 255:2], ident[:])
+        def mm_b(i, b):
+            t = bank("kb", "B%d" % i, b)
+            for tt in range(4):
+                nc.tensor.matmul_mx(out=col(t, tt), lhsT=col(buf("uc", b), tt).bitcast(FP8X4), lhsT_scale=col(buf("us", b), tt), rhs=col(buf("ac", b), i).bitcast(FP8X4), rhs_scale=col(buf("as", b), i), start=True, stop=True)
 
-        def pout(b):
-            evac("W", words_of(buf("pg", b)).rearrange("p (i m u) -> p i m u", i=2, u=2), made["P", b][:].rearrange("p (i u m) -> p i m u", i=2, u=2))
+        def pmul(i, b):
+            nc.vector.tensor_tensor(out=buf("pg", b)[:, P * i:P * i + P, :], in0=made["B%d" % i, b][:].rearrange("p (t m) -> p m t", t=4), in1=col(buf("arow", b), i).unsqueeze(2).to_broadcast([P, P, 4]), op=ALU.mult)
 
         def pquant(b):
             quantize(buf("pc", b)[:], col(pscale, b, M), buf("pg", b))
@@ -221,19 +225,24 @@ def tile_comireclabelawareinterests_x2_kernel(tc, h, w1_words, w1_scales, tb, g,
                 for q in range(4):
                     nc.sync.dma_start(out=out_2[0, 4 * q:4 * q + 4, :].bitcast(I32), in_=pscale[32 * q:32 * q + 4, :].bitcast(I32))
 
+        def quant_e(b):
+            quantize(buf("ec", b)[:], buf("es", b)[:], buf("eg", b))
+            if b == 0:
+                permute_ws()
+
         DO = {
             "Qh": lambda b: quantize(buf("hc", b)[:], buf("hs", b)[:], buf("hg", b)),
-            "Qe": lambda b: quantize(buf("ec", b)[:], buf("es", b)[:], buf("eg", b)),
+            "Qe": quant_e,
             "Qa": lambda b: quantize(buf("ac", b)[:], buf("as", b)[:], buf("ag", b)),
             "Qu": lambda b: quantize(buf("uc", b)[:], buf("us", b)[:], buf("ug", b)),
             "E": expo, "G": gain, "Z": zsum, "RZ": zrec, "ZR": zrow, "QR": qrow, "MN": qmin, "ER": erow, "EO": eown,
-            "RS": rsum, "AL": alpha, "W": pout, "Qp": pquant,
+            "RS": rsum, "AL": alpha, "AR": arow, "Qp": pquant,
         }
         for i in range(2):
             for x in "he":
                 DO["T%s%d" % (x, i)] = lambda b, x=x, i=i: turn(x, i, b)
                 DO["X%s%d" % (x, i)] = lambda b, x=x, i=i: unload(x, i, b)
-            for name, fn in (("K", mm_k), ("H", tanh), ("A", amul), ("V", mm_v), ("D", qdot), ("O", outp), ("R", rnd), ("P", pturn)):
+            for name, fn in (("K", mm_k), ("H", tanh), ("A", amul), ("V", mm_v), ("D", qdot), ("O", outp), ("B", mm_b), ("C", pmul)):
                 DO["%s%d" % (name, i)] = lambda b, fn=fn, i=i: fn(i, b)
         for q in range(4):
             DO["U%d" % q] = lambda b, q=q: mm_u(q, b)
@@ -242,19 +251,19 @@ def tile_comireclabelawareinterests_x2_kernel(tc, h, w1_words, w1_scales, tb, g,
         with tc.manual_schedule():
             load("h", h, 0)
             nc.vector.memset(w1s[:].bitcast(I32), 0)
-            nc.vector.memset(wss[:].bitcast(I32), 0)
+            nc.vector.memset(wss_in[:].bitcast(I32), 0)
             nc.gpsimd.memset(wg[:], 0.0)
             make_identity(nc, ident[:])
             nc.sync.dma_start(out=w1w[:].bitcast(I32), in_=w1_words[0].bitcast(I32))
             for q in range(4):
                 nc.sync.dma_start(out=w1s[32 * q:32 * q + 4, :].bitcast(I32), in_=w1_scales[0, 4 * q:4 * q + 4, :].bitcast(I32))
             load("e", e, 0)
-            nc.sync.dma_start(out=wsw[:].bitcast(I32), in_=ws_words[0].bitcast(I32))
+            nc.sync.dma_start(out=wsw_in[:].bitcast(I32), in_=ws_words[0].bitcast(I32))
             load("h", h, 1)
             nc.sync.dma_start(out=tb_sb[0:8, :], in_=tb[:, :])
             nc.sync.dma_start(out=g_sb[0:8, :], in_=g[:, :])
             for q in range(4):
-                nc.sync.dma_start(out=wss[32 * q:32 * q + 4, :].bitcast(I32), in_=ws_scales[0, 4 * q:4 * q + 4, :].bitcast(I32))
+                nc.sync.dma_start(out=wss_in[32 * q:32 * q + 4, :].bitcast(I32), in_=ws_scales[0, 4 * q:4 * q + 4, :].bitcast(I32))
             load("e", e, 1)
             load("h", h, 2)
             load("e", e, 2)

@@ -19,8 +19,8 @@ AF = mybir.ActivationFunctionType
 ALU = mybir.AluOpType
 AX = mybir.AxisListType
 
-STEPS = [("Xe1", 1), ("ZR", 2), ("D1", 3), ("D0", 3), ("Th0", 0), ("H0", 1), ("A0", 2), ("H1", 1), ("Xh0", 0), ("Th1", 0), ("A1", 2), ("U1", 2), ("U0", 2), ("E", 1), ("C0", 4), ("Y1", 2), ("Y0", 2), ("Xh1", 0), ("QR", 3), ("Te0", 1), ("MN", 3), ("Qp", 4), ("U3", 2), ("ER", 3), ("U2", 2), ("Te1", 0), ("G", 1), ("RS", 3), ("EO", 3), ("Qh", 0), ("Y3", 2), ("AR", 3), ("Qa", 2), ("Y2", 2), ("AL", 3), ("B1", 3), ("Xe0", 1), ("Qu", 2), ("O1", 3), ("Z", 1), ("K0", 0), ("C1", 3), ("Qe", 1), ("B0", 3), ("V1", 2), ("O0", 3), ("K1", 0), ("V0", 2), ("RZ", 1)]
-ENGINE = {"Xh0": "S", "Xh1": "V", "Xe0": "S", "Xe1": "S", "Y0": "S", "Y1": "S", "Y2": "S", "Y3": "S", "O0": "S", "O1": "S"}
+STEPS = [("V1", 4), ("O1", 5), ("K1", 1), ("Xe0", 2), ("ZR", 3), ("D1", 4), ("Th0", 0), ("H0", 1), ("V0", 4), ("H1", 1), ("A0", 3), ("A1", 3), ("U0", 3), ("D0", 4), ("U2", 3), ("Xh0", 0), ("Y0", 3), ("Qp", 5), ("Qe", 2), ("Th1", 0), ("Y2", 3), ("Xh1", 0), ("U1", 3), ("QR", 4), ("U3", 3), ("MN", 4), ("Y1", 3), ("ER", 4), ("S2", 2), ("G", 2), ("EO", 4), ("Qh", 0), ("RS", 4), ("Te1", 0), ("Y3", 3), ("Qa", 3), ("AL", 4), ("E", 1), ("B0", 4), ("Te0", 1), ("B1", 4), ("AR", 4), ("Qu", 3), ("C1", 4), ("Z", 2), ("K0", 0), ("O0", 4), ("RZ", 2), ("C0", 4), ("Xe1", 0), ("S1", 1)]
+ENGINE = {"Xh0": "S", "Xh1": "S", "Xe0": "S", "Xe1": "S", "Y0": "S", "Y1": "S", "Y2": "S", "Y3": "S", "O0": "S", "O1": "S"}
 
 
 def tile_comireclabelawareinterests_x2_kernel(tc, h, w1_words, w1_scales, tb, g, e, ws_words, ws_scales, c, out_0, out_1, out_2):
@@ -47,6 +47,7 @@ def tile_comireclabelawareinterests_x2_kernel(tc, h, w1_words, w1_scales, tb, g,
         wg = keep.tile([P, 2, S], F32, name="wg")
         cb = keep.tile([P, B, D], BF16, name="cb")
         wcol = keep.tile([P, 4, 2 * B], F32, name="wcol")
+        ones = keep.tile([P, 64], F32, name="ones")
         ident = keep.tile([P, P], F32, name="ident")
         pscale = keep.tile([P, B * M], U8, name="pscale", align_bytes=64)
 
@@ -54,7 +55,7 @@ def tile_comireclabelawareinterests_x2_kernel(tc, h, w1_words, w1_scales, tb, g,
             "h": ([P, 4, D], BF16, 6), "e": ([P, 4, D], BF16, 6),
             "hg": ([P, S, 4], BF16, 3), "eg": ([P, S, 4], BF16, 3),
             "hc": ([P, S], U32, 3), "ec": ([P, S], U32, 3), "hs": ([P, S], U8, 3), "es": ([P, S], U8, 3),
-            "tanh": ([P, 4, M], F32, 3), "ex": ([P, 4, M], F32, 3), "exg": ([P, 4, M], F32, 3),
+            "tanh": ([P, 4, M], F32, 3), "ex": ([P, 4, M], F32, 3), "exg": ([P, 4, M], F32, 3), "ep": ([P, 2, M], F32, 3), "et": ([P, M], F32, 3),
             "ag": ([P, M, 4], BF16, 3), "ac": ([P, M], U32, 4), "as": ([P, M], U8, 4),
             "ug": ([P, D, 4], BF16, 3), "uc": ([P, D], U32, 4), "us": ([P, D], U8, 4),
             "junk": ([P, D], F32, 2), "o": ([P, 2, D], F32, 4), "pg": ([P, M, 4], BF16, 3), "pc": ([P, M], U32, 4), "erow": ([P, M], F32, 3), "arow": ([P, M], F32, 3),
@@ -101,8 +102,8 @@ def tile_comireclabelawareinterests_x2_kernel(tc, h, w1_words, w1_scales, tb, g,
             nc.vector.tensor_reduce(out=mx[0:8, :], in_=tb_sb[0:8, :], axis=AX.X, op=ALU.max)
             nb = small.tile([P, 1], F32, name="nb")
             nc.vector.tensor_scalar(out=nb[0:8, :], in0=mx[0:8, :], scalar1=-1.0, scalar2=-2.0, op0=ALU.mult, op1=ALU.add)
-            nc.scalar.activation(out=wg[0:8, 0, :], in_=tb_sb[0:8, :], func=AF.Exp, bias=nb[0:8, :])
-            nc.vector.scalar_tensor_tensor(out=wg[0:8, 1, :], in0=g_sb[0:8, :], scalar=math.sqrt(S), in1=wg[0:8, 0, :], op0=ALU.mult, op1=ALU.mult)
+            nc.vector.tensor_scalar(out=wg[0:8, 0, :], in0=tb_sb[0:8, :], scalar1=nb[0:8, :], scalar2=None, op0=ALU.add)
+            nc.vector.tensor_scalar(out=wg[0:8, 1, :], in0=g_sb[0:8, :], scalar1=math.sqrt(S), scalar2=None, op0=ALU.mult)
             for r in range(2):
                 wbank = bank("bank", "wbank", r)
                 for t in range(4):
@@ -140,17 +141,23 @@ def tile_comireclabelawareinterests_x2_kernel(tc, h, w1_words, w1_scales, tb, g,
         def expo(b):
             if b == 0:
                 token_weights()
-            nc.scalar.activation(out=buf("ex", b)[:], in_=buf("tanh", b)[:], func=AF.Exp, scale=2.0)
+            for t in range(4):
+                nc.scalar.activation(out=buf("ex", b)[:, t, :], in_=buf("tanh", b)[:, t, :], func=AF.Exp, scale=2.0, bias=wcol[:, t, b:b + 1])
 
         def gain(b):
             for t in range(4):
                 nc.vector.tensor_scalar(out=buf("exg", b)[:, t, :], in0=buf("ex", b)[:, t, :], scalar1=wcol[:, t, B + b:B + b + 1], scalar2=None, op0=ALU.mult)
 
+        def esum1(b):
+            nc.vector.tensor_tensor(out=buf("ep", b)[:], in0=buf("ex", b)[:, 0:2, :], in1=buf("ex", b)[:, 2:4, :], op=ALU.add)
+
+        def esum2(b):
+            nc.vector.tensor_tensor(out=buf("et", b)[:], in0=buf("ep", b)[:, 0, :], in1=buf("ep", b)[:, 1, :], op=ALU.add)
+
         def zsum(b):
             zt = bank("sm", "Z", b)
             for i in range(2):
-                for t in range(4):
-                    nc.tensor.matmul(zt[:, 64 * i:64 * i + 64], lhsT=buf("ex", b)[:, t, P * i:P * i + P], rhs=wcol[:, t, b:b + 1].to_broadcast([P, 64]), start=(t == 0), stop=(t == 3))
+                nc.tensor.matmul(zt[:, 64 * i:64 * i + 64], lhsT=col(buf("et", b), i), rhs=ones[:], start=True, stop=True)
 
         def zrec(b):
             nc.vector.reciprocal(out=buf("rz", b)[:], in_=made["Z", b][:, 0:65:64])
@@ -235,7 +242,7 @@ def tile_comireclabelawareinterests_x2_kernel(tc, h, w1_words, w1_scales, tb, g,
             "Qe": quant_e,
             "Qa": lambda b: quantize(buf("ac", b)[:], buf("as", b)[:], buf("ag", b)),
             "Qu": lambda b: quantize(buf("uc", b)[:], buf("us", b)[:], buf("ug", b)),
-            "E": expo, "G": gain, "Z": zsum, "RZ": zrec, "ZR": zrow, "QR": qrow, "MN": qmin, "ER": erow, "EO": eown,
+            "E": expo, "S1": esum1, "S2": esum2, "G": gain, "Z": zsum, "RZ": zrec, "ZR": zrow, "QR": qrow, "MN": qmin, "ER": erow, "EO": eown,
             "RS": rsum, "AL": alpha, "AR": arow, "Qp": pquant,
         }
         for i in range(2):
@@ -253,6 +260,7 @@ def tile_comireclabelawareinterests_x2_kernel(tc, h, w1_words, w1_scales, tb, g,
             nc.vector.memset(w1s[:].bitcast(I32), 0)
             nc.vector.memset(wss_in[:].bitcast(I32), 0)
             nc.gpsimd.memset(wg[:], 0.0)
+            nc.vector.memset(ones[:], 1.0)
             make_identity(nc, ident[:])
             nc.sync.dma_start(out=w1w[:].bitcast(I32), in_=w1_words[0].bitcast(I32))
             for q in range(4):
@@ -267,12 +275,13 @@ def tile_comireclabelawareinterests_x2_kernel(tc, h, w1_words, w1_scales, tb, g,
             load("e", e, 1)
             load("h", h, 2)
             load("e", e, 2)
-            nc.sync.dma_start(out=cb[:].rearrange("p b j -> p (b j)"), in_=c.rearrange("b j -> (b j)").partition_broadcast(P))
             last = max(lag for step, lag in STEPS)
             for n in range(B + last):
                 if 3 <= n + 3 < B:
                     load("h", h, n + 3)
                     load("e", e, n + 3)
+                if n == 0:
+                    nc.sync.dma_start(out=cb[:].rearrange("p b j -> p (b j)"), in_=c.rearrange("b j -> (b j)").partition_broadcast(P))
                 for step, lag in STEPS:
                     if 0 <= n - lag < B:
                         DO[step](n - lag)

@@ -6,6 +6,7 @@ from concourse.masks import make_identity
 
 B, S, D, M = 8, 512, 512, 256
 P = 128
+T = 4
 FLOPS = 2 * B * (S * D * M + S * D * D + M * S * D)
 
 F32 = mybir.dt.float32
@@ -15,273 +16,402 @@ U32 = mybir.dt.uint32
 U8 = mybir.dt.uint8
 FP8X4 = mybir.dt.float8_e4m3fn_x4
 FP4X4 = mybir.dt.float4_e2m1fn_x4
-AF = mybir.ActivationFunctionType
+ACT = mybir.ActivationFunctionType
 ALU = mybir.AluOpType
-AX = mybir.AxisListType
+AXIS_X = mybir.AxisListType.X
 
-STEPS = [("V1", 4), ("O1", 5), ("K1", 1), ("Xe0", 2), ("ZR", 3), ("D1", 4), ("Th0", 0), ("H0", 1), ("V0", 4), ("H1", 1), ("A0", 3), ("A1", 3), ("U0", 3), ("D0", 4), ("U2", 3), ("Xh0", 0), ("Y0", 3), ("Qp", 5), ("Qe", 2), ("Th1", 0), ("Y2", 3), ("Xh1", 0), ("U1", 3), ("QR", 4), ("U3", 3), ("MN", 4), ("Y1", 3), ("ER", 4), ("S2", 2), ("G", 2), ("EO", 4), ("Qh", 0), ("RS", 4), ("Te1", 0), ("Y3", 3), ("Qa", 3), ("AL", 4), ("E", 1), ("B0", 4), ("Te0", 1), ("B1", 4), ("AR", 4), ("Qu", 3), ("C1", 4), ("Z", 2), ("K0", 0), ("O0", 4), ("RZ", 2), ("C0", 4), ("Xe1", 0), ("S1", 1)]
-ENGINE = {"Xh0": "S", "Xh1": "S", "Xe0": "S", "Xe1": "S", "Y0": "S", "Y1": "S", "Y2": "S", "Y3": "S", "O0": "S", "O1": "S"}
+SUM_COLUMNS = 64
+AHEAD = 3
+
+PERIOD = (
+    ("pool1", 4), ("output1", 5), ("score1", 1), ("unload_e0", 2), ("spread_inverse", 3), ("dot1", 4),
+    ("turn_h0", 0), ("tanh0", 1), ("pool0", 4), ("tanh1", 1), ("weigh0", 3), ("weigh1", 3), ("project0", 3),
+    ("dot0", 4), ("project2", 3), ("unload_h0", 0), ("unload_u0", 3), ("quantize_p", 5), ("quantize_e", 2),
+    ("turn_h1", 0), ("unload_u2", 3), ("unload_h1", 0), ("project1", 3), ("spread_q", 4), ("project3", 3),
+    ("min_q", 4), ("unload_u1", 3), ("exp_row", 4), ("fold_all", 2), ("gain", 2), ("exp_own", 4),
+    ("quantize_h", 0), ("invert_total", 4), ("turn_e1", 0), ("unload_u3", 3), ("quantize_a", 3),
+    ("alpha_own", 4), ("exp", 1), ("pool_turned0", 4), ("turn_e0", 1), ("pool_turned1", 4), ("alpha_row", 4),
+    ("quantize_u", 3), ("reweigh1", 4), ("sum_tokens", 2), ("score0", 0), ("output0", 4), ("invert_sums", 2),
+    ("reweigh0", 4), ("unload_e1", 0), ("fold_pairs", 1),
+)
 
 
-def tile_comireclabelawareinterests_x2_kernel(tc, h, w1_words, w1_scales, tb, g, e, ws_words, ws_scales, c, out_0, out_1, out_2):
+def tile_comireclabelawareinterests_x2_kernel(
+    tc, h, w1_words, w1_scales, tb, g, e, ws_words, ws_scales, c, out_0, out_1, out_2
+):
     nc = tc.nc
+    source = {"h": h, "e": e}
+
     with ExitStack() as ctx:
         keep = ctx.enter_context(tc.tile_pool(name="keep", bufs=1))
         work = ctx.enter_context(tc.tile_pool(name="work", bufs=3))
-        small = ctx.enter_context(tc.tile_pool(name="small", bufs=4))
-        pools = {
-            "bank": (ctx.enter_context(tc.psum_pool(name="ps_t", bufs=2)), 512),
-            "kb": (ctx.enter_context(tc.psum_pool(name="ps_k", bufs=3)), 512),
-            "v": (ctx.enter_context(tc.psum_pool(name="ps_v", bufs=2)), 512),
-            "sm": (ctx.enter_context(tc.psum_pool(name="ps_s", bufs=1)), 512),
+        banks = {
+            "turn": ctx.enter_context(tc.psum_pool(name="ps_turn", bufs=2)),
+            "product": ctx.enter_context(tc.psum_pool(name="ps_product", bufs=3)),
+            "v": ctx.enter_context(tc.psum_pool(name="ps_v", bufs=2)),
+            "row": ctx.enter_context(tc.psum_pool(name="ps_row", bufs=1)),
         }
 
-        w1w = keep.tile([P, 2 * M], U8, name="w1w", align_bytes=64)
-        w1s = keep.tile([P, M], U8, name="w1s", align_bytes=64)
-        wsw = keep.tile([P, 2 * D], U8, name="wsw", align_bytes=64)
-        wss = keep.tile([P, D], U8, name="wss", align_bytes=64)
-        wsw_in = keep.tile([P, 2 * D], U8, name="wsw_in", align_bytes=64)
-        wss_in = keep.tile([P, D], U8, name="wss_in", align_bytes=64)
-        tb_sb = keep.tile([P, S], BF16, name="tb_sb")
-        g_sb = keep.tile([P, S], BF16, name="g_sb")
-        wg = keep.tile([P, 2, S], F32, name="wg")
-        cb = keep.tile([P, B, D], BF16, name="cb")
-        wcol = keep.tile([P, 4, 2 * B], F32, name="wcol")
-        ones = keep.tile([P, 64], F32, name="ones")
-        ident = keep.tile([P, P], F32, name="ident")
-        pscale = keep.tile([P, B * M], U8, name="pscale", align_bytes=64)
+        w1_codes = keep.tile([P, 2 * M], U8, name="w1_codes", align_bytes=64)
+        w1_scale = keep.tile([P, M], U8, name="w1_scale", align_bytes=64)
+        ws_loaded = keep.tile([P, 2 * D], U8, name="ws_loaded", align_bytes=64)
+        ws_scale_loaded = keep.tile([P, D], U8, name="ws_scale_loaded", align_bytes=64)
+        ws_codes = keep.tile([P, 2 * D], U8, name="ws_codes", align_bytes=64)
+        ws_scale = keep.tile([P, D], U8, name="ws_scale", align_bytes=64)
+        tb_rows = keep.tile([P, S], BF16, name="tb_rows")
+        g_rows = keep.tile([P, S], BF16, name="g_rows")
+        token_rows = keep.tile([P, 2, S], F32, name="token_rows")
+        token_cols = keep.tile([P, T, 2 * B], F32, name="token_cols")
+        c_all = keep.tile([P, B, D], BF16, name="c_all")
+        ones = keep.tile([P, SUM_COLUMNS], F32, name="ones")
+        identity = keep.tile([P, P], F32, name="identity")
+        p_scale = keep.tile([P, B * M], U8, name="p_scale", align_bytes=64)
 
-        SPEC = {
-            "h": ([P, 4, D], BF16, 6), "e": ([P, 4, D], BF16, 6),
-            "hg": ([P, S, 4], BF16, 3), "eg": ([P, S, 4], BF16, 3),
-            "hc": ([P, S], U32, 3), "ec": ([P, S], U32, 3), "hs": ([P, S], U8, 3), "es": ([P, S], U8, 3),
-            "tanh": ([P, 4, M], F32, 3), "ex": ([P, 4, M], F32, 3), "exg": ([P, 4, M], F32, 3), "ep": ([P, 2, M], F32, 3), "et": ([P, M], F32, 3),
-            "ag": ([P, M, 4], BF16, 3), "ac": ([P, M], U32, 4), "as": ([P, M], U8, 4),
-            "ug": ([P, D, 4], BF16, 3), "uc": ([P, D], U32, 4), "us": ([P, D], U8, 4),
-            "junk": ([P, D], F32, 2), "o": ([P, 2, D], F32, 4), "pg": ([P, M, 4], BF16, 3), "pc": ([P, M], U32, 4), "erow": ([P, M], F32, 3), "arow": ([P, M], F32, 3),
-            "rz": ([P, 2], F32, 4), "qn": ([P, 2], F32, 4), "mn": ([P, 1], F32, 4), "esum": ([P, 1], F32, 4),
-            "eown": ([P, 2], F32, 4), "rs": ([P, 1], F32, 4), "alpha": ([P, 2], F32, 4),
+        shapes = {
+            "h": ([P, T, D], BF16, 6), "e": ([P, T, D], BF16, 6),
+            "h_grouped": ([P, S, T], BF16, 3), "e_grouped": ([P, S, T], BF16, 3),
+            "h_codes": ([P, S], U32, 3), "e_codes": ([P, S], U32, 3),
+            "h_scale": ([P, S], U8, 3), "e_scale": ([P, S], U8, 3),
+            "tanh": ([P, T, M], F32, 3), "exp": ([P, T, M], F32, 3), "gained": ([P, T, M], F32, 3),
+            "pair_sum": ([P, 2, M], F32, 3), "token_sum": ([P, M], F32, 3), "inverse": ([P, 2], F32, 4),
+            "a_grouped": ([P, M, T], BF16, 3), "a_codes": ([P, M], U32, 4), "a_scale": ([P, M], U8, 4),
+            "u_grouped": ([P, D, T], BF16, 3), "u_codes": ([P, D], U32, 4), "u_scale": ([P, D], U8, 4),
+            "minus_q": ([P, 2], F32, 4), "min_q": ([P, 1], F32, 4), "total": ([P, 1], F32, 4),
+            "exp_row": ([P, M], F32, 3), "exp_own": ([P, 2], F32, 4), "inverse_total": ([P, 1], F32, 4),
+            "alpha_own": ([P, 2], F32, 4), "alpha_row": ([P, M], F32, 3),
+            "out": ([P, 2, D], F32, 4), "p_grouped": ([P, M, T], BF16, 3), "p_codes": ([P, M], U32, 4),
         }
-        made = {}
+        live = {}
 
         def buf(name, b):
-            if (name, b) not in made:
-                shape, dtype, bufs = SPEC[name]
-                t = work.tile(shape, dtype, name=name, bufs=bufs, align_bytes=64)
-                made[name, b] = t
-            return made[name, b]
+            if (name, b) not in live:
+                shape, dtype, bufs = shapes[name]
+                live[name, b] = work.tile(shape, dtype, name=name, bufs=bufs, align_bytes=64)
+            return live[name, b]
 
-        def bank(pool, name, b):
-            t = pools[pool][0].tile([P, 512], F32, name=pool)
-            made[name, b] = t
-            return t
+        def new_bank(kind, name, b):
+            live[name, b] = banks[kind].tile([P, 512], F32, name=kind)
+            return live[name, b]
 
-        def load(name, src, b):
-            t = buf(name, b)
-            v = src[b].rearrange("(p t) f -> p t f", t=4)
-            if b == 0:
-                nc.sync.dma_start(out=t[:, 0:2, :], in_=v[:, 0:2, :])
-                nc.sync.dma_start(out=t[:, 2:4, :], in_=v[:, 2:4, :])
-            else:
-                nc.sync.dma_start(out=t[:], in_=v)
+        def part(ap, i, width=P):
+            return ap[:, width * i : width * i + width]
 
-        def evac(step, dst, src):
-            if ENGINE[step] == "V":
-                nc.vector.tensor_copy(out=dst, in_=src)
-            else:
-                nc.scalar.copy(out=dst, in_=src)
+        def as_words(ap):
+            return ap[:].rearrange("p x y -> p (x y)").bitcast(F32)
 
-        def words_of(t):
-            return t[:].rearrange("p a k -> p (a k)").bitcast(F32)
+        def by_four(ap):
+            return ap.rearrange("p t (n i) -> p n t i", i=4)
 
-        def col(t, i, n=P):
-            return t[:, n * i:n * i + n]
+        def grouped_by_four(ap):
+            return ap.rearrange("p (n i) t -> p n t i", i=4)
 
-        def token_weights():
-            mx = small.tile([P, 1], F32, name="mx")
-            nc.vector.tensor_reduce(out=mx[0:8, :], in_=tb_sb[0:8, :], axis=AX.X, op=ALU.max)
-            nb = small.tile([P, 1], F32, name="nb")
-            nc.vector.tensor_scalar(out=nb[0:8, :], in0=mx[0:8, :], scalar1=-1.0, scalar2=-2.0, op0=ALU.mult, op1=ALU.add)
-            nc.vector.tensor_scalar(out=wg[0:8, 0, :], in0=tb_sb[0:8, :], scalar1=nb[0:8, :], scalar2=None, op0=ALU.add)
-            nc.vector.tensor_scalar(out=wg[0:8, 1, :], in0=g_sb[0:8, :], scalar1=math.sqrt(S), scalar2=None, op0=ALU.mult)
+        def row_by_four(row):
+            return row.rearrange("p (n i) -> p n i", i=4).unsqueeze(2).to_broadcast([P, P // 4, T, 4])
+
+
+        def load(name, b):
+            tile = buf(name, b)
+            rows = source[name][b].rearrange("(p t) f -> p t f", t=T)
+            pieces = 2 if b == 0 else 1
+            for i in range(pieces):
+                ts = slice(i * T // pieces, (i + 1) * T // pieces)
+                nc.sync.dma_start(out=tile[:, ts, :], in_=rows[:, ts, :])
+
+        def load_scale(tile, scales):
+            for quad in range(4):
+                nc.sync.dma_start(
+                    out=tile[32 * quad : 32 * quad + 4, :].bitcast(I32),
+                    in_=scales[0, 4 * quad : 4 * quad + 4, :].bitcast(I32),
+                )
+
+        def token_columns():
+            largest = work.tile([P, 1], F32, name="largest", bufs=1)
+            nc.vector.tensor_reduce(out=largest[0:B, :], in_=tb_rows[0:B, :], axis=AXIS_X, op=ALU.max)
+            shift = work.tile([P, 1], F32, name="shift", bufs=1)
+            nc.vector.tensor_scalar(
+                out=shift[0:B, :], in0=largest[0:B, :], scalar1=-1.0, scalar2=-2.0, op0=ALU.mult, op1=ALU.add
+            )
+            nc.vector.tensor_scalar(
+                out=token_rows[0:B, 0, :], in0=tb_rows[0:B, :], scalar1=shift[0:B, :], scalar2=None, op0=ALU.add
+            )
+            nc.vector.tensor_scalar(
+                out=token_rows[0:B, 1, :], in0=g_rows[0:B, :], scalar1=math.sqrt(S), scalar2=None, op0=ALU.mult
+            )
             for r in range(2):
-                wbank = bank("bank", "wbank", r)
-                for t in range(4):
-                    nc.tensor.transpose(col(wbank, t), wg[:, r, t:t + 509:4], ident[:])
-                nc.vector.tensor_copy(out=wcol[:, :, B * r:B * r + B], in_=wbank[:].rearrange("p (t n) -> p t n", t=4)[:, :, 0:B])
+                bank = new_bank("turn", "token_rows", r)
+                for t in range(T):
+                    nc.tensor.transpose(part(bank, t), token_rows[:, r, t : t + S - T + 1 : T], identity[:])
+                nc.vector.tensor_copy(
+                    out=token_cols[:, :, B * r : B * r + B],
+                    in_=bank[:].rearrange("p (t n) -> p t n", t=T)[:, :, 0:B],
+                )
 
         def permute_ws():
-            nc.vector.tensor_copy(out=wss[:].rearrange("p (t m) -> p m t", t=4), in_=wss_in[:].rearrange("p (m t) -> p m t", t=4))
-            nc.vector.tensor_copy(out=wsw[:].rearrange("p (t m b) -> p m t b", t=4, b=2), in_=wsw_in[:].rearrange("p (m t b) -> p m t b", t=4, b=2))
+            nc.vector.tensor_copy(
+                out=ws_scale[:].rearrange("p (t m) -> p m t", t=T),
+                in_=ws_scale_loaded[:].rearrange("p (m t) -> p m t", t=T),
+            )
+            nc.vector.tensor_copy(
+                out=ws_codes[:].rearrange("p (t m y) -> p m t y", t=T, y=2),
+                in_=ws_loaded[:].rearrange("p (m t y) -> p m t y", t=T, y=2),
+            )
 
-        def turn(x, half, b):
-            t = bank("bank", "T%s%d" % (x, half), b)
-            words = words_of(buf(x, b))
+
+        def turn(name, half, b):
+            bank = new_bank("turn", "turn_%s%d" % (name, half), b)
+            words = as_words(buf(name, b))
             for tt in range(2):
-                for u in range(2):
-                    w0 = 256 * (2 * half + tt) + u
-                    nc.tensor.transpose(col(t, 2 * tt + u), words[:, w0:w0 + 255:2], ident[:])
+                for y in range(2):
+                    first = (2 * half + tt) * (D // 2) + y
+                    nc.tensor.transpose(part(bank, 2 * tt + y), words[:, first : first + D // 2 - 1 : 2], identity[:])
 
-        def unload(x, half, b):
-            dst = words_of(buf(x + "g", b)).rearrange("p (s u) -> p s u", u=2)[:, 256 * half:256 * half + 256, :]
-            evac("X%s%d" % (x, half), dst.rearrange("p (t r) u -> p t r u", t=2), made["T%s%d" % (x, half), b][:].rearrange("p (t u r) -> p t r u", t=2, u=2))
+        def unload_turned(name, half, b):
+            words = as_words(buf(name + "_grouped", b)).rearrange("p (s y) -> p s y", y=2)
+            nc.scalar.copy(
+                out=words[:, 2 * P * half : 2 * P * half + 2 * P, :].rearrange("p (t r) y -> p t r y", t=2),
+                in_=live["turn_%s%d" % (name, half), b][:].rearrange("p (t y r) -> p t r y", t=2, y=2),
+            )
 
-        def quantize(codes, scales, src):
-            nc.vector.quantize_mx(out=codes.bitcast(FP8X4), scales=scales, in_=src[:].rearrange("p a k -> p (a k)"))
+        def quantize(name, b, scale):
+            nc.vector.quantize_mx(
+                out=buf(name + "_codes", b)[:].bitcast(FP8X4),
+                scales=scale,
+                in_=buf(name + "_grouped", b)[:].rearrange("p n t -> p (n t)"),
+            )
 
-        def mm_k(half, b):
-            t = bank("kb", "K%d" % half, b)
-            for tt in range(2):
-                cols = slice(P * (2 * half + tt), P * (2 * half + tt + 1))
-                nc.tensor.matmul_mx(out=col(t, tt, M), lhsT=buf("hc", b)[:, cols].bitcast(FP8X4), lhsT_scale=buf("hs", b)[:, cols], rhs=w1w[:].bitcast(FP4X4), rhs_scale=w1s[:], start=True, stop=True)
-
-        def tanh(half, b):
-            nc.scalar.activation(out=buf("tanh", b)[:, 2 * half:2 * half + 2, :], in_=made["K%d" % half, b][:].rearrange("p (t m) -> p t m", t=2), func=AF.Tanh)
-
-        def expo(b):
-            if b == 0:
-                token_weights()
-            for t in range(4):
-                nc.scalar.activation(out=buf("ex", b)[:, t, :], in_=buf("tanh", b)[:, t, :], func=AF.Exp, scale=2.0, bias=wcol[:, t, b:b + 1])
-
-        def gain(b):
-            for t in range(4):
-                nc.vector.tensor_scalar(out=buf("exg", b)[:, t, :], in0=buf("ex", b)[:, t, :], scalar1=wcol[:, t, B + b:B + b + 1], scalar2=None, op0=ALU.mult)
-
-        def esum1(b):
-            nc.vector.tensor_tensor(out=buf("ep", b)[:], in0=buf("ex", b)[:, 0:2, :], in1=buf("ex", b)[:, 2:4, :], op=ALU.add)
-
-        def esum2(b):
-            nc.vector.tensor_tensor(out=buf("et", b)[:], in0=buf("ep", b)[:, 0, :], in1=buf("ep", b)[:, 1, :], op=ALU.add)
-
-        def zsum(b):
-            zt = bank("sm", "Z", b)
-            for i in range(2):
-                nc.tensor.matmul(zt[:, 64 * i:64 * i + 64], lhsT=col(buf("et", b), i), rhs=ones[:], start=True, stop=True)
-
-        def zrec(b):
-            nc.vector.reciprocal(out=buf("rz", b)[:], in_=made["Z", b][:, 0:65:64])
-
-        def zrow(b):
-            for i in range(2):
-                nc.tensor.transpose(col(made["Z", b], 2 + i), buf("rz", b)[:, i:i + 1].to_broadcast([P, P]), ident[:])
-
-        def amul(i, b):
-            ms = slice(P * i, P * i + P)
-            nc.vector.tensor_tensor(out=buf("ag", b)[:, ms, :], in0=buf("exg", b)[:, :, ms].rearrange("p t m -> p m t"), in1=col(made["Z", b], 2 + i).unsqueeze(2).to_broadcast([P, P, 4]), op=ALU.mult)
-
-        def mm_u(q, b):
-            t = bank("kb", "U%d" % q, b)
-            for tt in range(4):
-                nc.tensor.matmul_mx(out=col(t, tt), lhsT=col(buf("ec", b), tt).bitcast(FP8X4), lhsT_scale=col(buf("es", b), tt), rhs=wsw[:, 256 * q:256 * q + 256].bitcast(FP4X4), rhs_scale=col(wss, q), start=True, stop=True)
-
-        def uout(q, b):
-            evac("Y%d" % q, buf("ug", b)[:, P * q:P * q + P, :], made["U%d" % q, b][:].rearrange("p (t j) -> p j t", t=4))
-
-        def mm_v(i, b):
-            v = bank("v", "V%d" % i, b)
-            nc.tensor.matmul_mx(out=v[:], lhsT=col(buf("ac", b), i).bitcast(FP8X4), lhsT_scale=col(buf("as", b), i), rhs=buf("uc", b)[:].bitcast(FP8X4), rhs_scale=buf("us", b)[:], start=True, stop=True)
-
-        def qdot(i, b):
-            junk = work.tile([P, D], F32, name="junk", bufs=2, align_bytes=64)
-            nc.vector.scalar_tensor_tensor(out=junk[:].rearrange("p (m t) -> p m t", t=4), in0=made["V%d" % i, b][:].rearrange("p (t m) -> p m t", t=4), scalar=-1.0 / math.sqrt(D), in1=cb[:, b, :].rearrange("p (m t) -> p m t", t=4), op0=ALU.mult, op1=ALU.mult, accum_out=buf("qn", b)[:, i:i + 1])
-
-        def qrow(b):
-            t = bank("sm", "Q", b)
-            for i in range(2):
-                nc.tensor.transpose(col(t, i), buf("qn", b)[:, i:i + 1].to_broadcast([P, P]), ident[:])
-
-        def qmin(b):
-            nc.vector.tensor_reduce(out=buf("mn", b)[:], in_=made["Q", b][:, 0:M], axis=AX.X, op=ALU.min)
-
-        def erow(b):
-            nc.scalar.activation(out=buf("erow", b)[:], in_=made["Q", b][:, 0:M], func=AF.Exp, scale=-1.0, bias=buf("mn", b)[:], accum_out=buf("esum", b)[:])
-
-        def eown(b):
-            nc.scalar.activation(out=buf("eown", b)[:], in_=buf("qn", b)[:], func=AF.Exp, scale=-1.0, bias=buf("mn", b)[:])
-
-        def rsum(b):
-            nc.vector.reciprocal(out=buf("rs", b)[:], in_=buf("esum", b)[:])
-
-        def alpha(b):
-            nc.vector.tensor_scalar(out=buf("alpha", b)[:], in0=buf("eown", b)[:], scalar1=buf("rs", b)[:], scalar2=float(M), op0=ALU.mult, op1=ALU.mult)
-
-        def outp(i, b):
-            o = buf("o", b)
-            if ENGINE["O%d" % i] == "V":
-                nc.vector.tensor_scalar(out=o[:, i, :].rearrange("p (m t) -> p m t", t=4), in0=made["V%d" % i, b][:].rearrange("p (t m) -> p m t", t=4), scalar1=buf("alpha", b)[:, i:i + 1], scalar2=None, op0=ALU.mult)
-            else:
-                nc.scalar.activation(out=o[:, i, :].rearrange("p (m t) -> p m t", t=4), in_=made["V%d" % i, b][:].rearrange("p (t m) -> p m t", t=4), func=AF.Copy, scale=buf("alpha", b)[:, i:i + 1])
-            nc.sync.dma_start(out=out_0[b, P * i:P * i + P, :], in_=o[:, i, :])
-
-        def arow(b):
-            nc.vector.tensor_scalar(out=buf("arow", b)[:], in0=buf("erow", b)[:], scalar1=buf("rs", b)[:], scalar2=float(M), op0=ALU.mult, op1=ALU.mult)
-
-        def mm_b(i, b):
-            t = bank("kb", "B%d" % i, b)
-            for tt in range(4):
-                nc.tensor.matmul_mx(out=col(t, tt), lhsT=col(buf("uc", b), tt).bitcast(FP8X4), lhsT_scale=col(buf("us", b), tt), rhs=col(buf("ac", b), i).bitcast(FP8X4), rhs_scale=col(buf("as", b), i), start=True, stop=True)
-
-        def pmul(i, b):
-            nc.vector.tensor_tensor(out=buf("pg", b)[:, P * i:P * i + P, :], in0=made["B%d" % i, b][:].rearrange("p (t m) -> p m t", t=4), in1=col(buf("arow", b), i).unsqueeze(2).to_broadcast([P, P, 4]), op=ALU.mult)
-
-        def pquant(b):
-            quantize(buf("pc", b)[:], col(pscale, b, M), buf("pg", b))
-            nc.sync.dma_start(out=out_1[0, :, M * b:M * b + M, :].rearrange("p m t -> p (m t)").bitcast(I32), in_=buf("pc", b)[:].bitcast(I32))
-            if b == B - 1:
-                for q in range(4):
-                    nc.sync.dma_start(out=out_2[0, 4 * q:4 * q + 4, :].bitcast(I32), in_=pscale[32 * q:32 * q + 4, :].bitcast(I32))
-
-        def quant_e(b):
-            quantize(buf("ec", b)[:], buf("es", b)[:], buf("eg", b))
-            if b == 0:
+        def quantize_operand(name, b):
+            quantize(name, b, buf(name + "_scale", b)[:])
+            if name == "e" and b == 0:
                 permute_ws()
 
-        DO = {
-            "Qh": lambda b: quantize(buf("hc", b)[:], buf("hs", b)[:], buf("hg", b)),
-            "Qe": quant_e,
-            "Qa": lambda b: quantize(buf("ac", b)[:], buf("as", b)[:], buf("ag", b)),
-            "Qu": lambda b: quantize(buf("uc", b)[:], buf("us", b)[:], buf("ug", b)),
-            "E": expo, "S1": esum1, "S2": esum2, "G": gain, "Z": zsum, "RZ": zrec, "ZR": zrow, "QR": qrow, "MN": qmin, "ER": erow, "EO": eown,
-            "RS": rsum, "AL": alpha, "AR": arow, "Qp": pquant,
+        def multiply(out, name, i, b, rhs, rhs_scale):
+            nc.tensor.matmul_mx(
+                out=out,
+                lhsT=part(buf(name + "_codes", b), i).bitcast(FP8X4),
+                lhsT_scale=part(buf(name + "_scale", b), i),
+                rhs=rhs,
+                rhs_scale=rhs_scale,
+                start=True,
+                stop=True,
+            )
+
+
+        def score(half, b):
+            bank = new_bank("product", "score%d" % half, b)
+            for tt in range(2):
+                multiply(part(bank, tt, M), "h", 2 * half + tt, b, w1_codes[:].bitcast(FP4X4), w1_scale[:])
+
+        def tanh(half, b):
+            nc.scalar.activation(
+                out=buf("tanh", b)[:, 2 * half : 2 * half + 2, :],
+                in_=live["score%d" % half, b][:].rearrange("p (t m) -> p t m", t=2),
+                func=ACT.Tanh,
+            )
+
+        def exponential(b):
+            if b == 0:
+                token_columns()
+            for t in range(T):
+                nc.scalar.activation(
+                    out=buf("exp", b)[:, t, :],
+                    in_=buf("tanh", b)[:, t, :],
+                    func=ACT.Exp,
+                    scale=2.0,
+                    bias=token_cols[:, t, b : b + 1],
+                )
+
+        def fold_pairs(b):
+            x = buf("exp", b)
+            nc.vector.tensor_tensor(out=buf("pair_sum", b)[:], in0=x[:, 0:2, :], in1=x[:, 2:4, :], op=ALU.add)
+
+        def fold_all(b):
+            x = buf("pair_sum", b)
+            nc.vector.tensor_tensor(out=buf("token_sum", b)[:], in0=x[:, 0, :], in1=x[:, 1, :], op=ALU.add)
+
+        def sum_tokens(b):
+            bank = new_bank("row", "sums", b)
+            for i in range(2):
+                nc.tensor.matmul(
+                    part(bank, i, SUM_COLUMNS), lhsT=part(buf("token_sum", b), i), rhs=ones[:], start=True, stop=True
+                )
+
+        def invert_sums(b):
+            first_columns = live["sums", b][:, 0 : SUM_COLUMNS + 1 : SUM_COLUMNS]
+            nc.vector.reciprocal(out=buf("inverse", b)[:], in_=first_columns)
+
+        def spread(bank, first, column_pair):
+            for i in range(2):
+                nc.tensor.transpose(
+                    part(bank, first + i), column_pair[:, i : i + 1].to_broadcast([P, P]), identity[:]
+                )
+
+        def spread_inverse(b):
+            spread(live["sums", b], 2, buf("inverse", b))
+
+        def gain(b):
+            for t in range(T):
+                nc.vector.tensor_scalar(
+                    out=buf("gained", b)[:, t, :],
+                    in0=buf("exp", b)[:, t, :],
+                    scalar1=token_cols[:, t, B + b : B + b + 1],
+                    scalar2=None,
+                    op0=ALU.mult,
+                )
+
+        def weigh(i, b):
+            ms = slice(P * i, P * i + P)
+            nc.vector.tensor_tensor(
+                out=grouped_by_four(buf("a_grouped", b)[:, ms, :]),
+                in0=by_four(buf("gained", b)[:, :, ms]),
+                in1=row_by_four(part(live["sums", b], 2 + i)),
+                op=ALU.mult,
+            )
+
+
+        def project(i, b):
+            bank = new_bank("product", "project%d" % i, b)
+            for t in range(T):
+                multiply(part(bank, t), "e", t, b, part(ws_codes, i, 2 * P).bitcast(FP4X4), part(ws_scale, i))
+
+        def unload_u(i, b):
+            nc.scalar.copy(
+                out=grouped_by_four(buf("u_grouped", b)[:, P * i : P * i + P, :]),
+                in_=by_four(live["project%d" % i, b][:].rearrange("p (t n) -> p t n", t=T)),
+            )
+
+
+        def pool(i, b):
+            bank = new_bank("v", "pool%d" % i, b)
+            multiply(bank[:], "a", i, b, buf("u_codes", b)[:].bitcast(FP8X4), buf("u_scale", b)[:])
+
+        def dot(i, b):
+            products = work.tile([P, D], F32, name="products", bufs=2, align_bytes=64)
+            nc.vector.scalar_tensor_tensor(
+                out=products[:].rearrange("p (t m) -> p t m", t=T),
+                in0=live["pool%d" % i, b][:].rearrange("p (t m) -> p t m", t=T),
+                scalar=-1.0 / math.sqrt(D),
+                in1=c_all[:, b, :].rearrange("p (m t) -> p t m", t=T),
+                op0=ALU.mult,
+                op1=ALU.mult,
+                accum_out=buf("minus_q", b)[:, i : i + 1],
+            )
+
+        def spread_q(b):
+            spread(new_bank("row", "q", b), 0, buf("minus_q", b))
+
+        def min_q(b):
+            nc.vector.tensor_reduce(out=buf("min_q", b)[:], in_=live["q", b][:, 0:M], axis=AXIS_X, op=ALU.min)
+
+        def exp_row(b):
+            nc.scalar.activation(
+                out=buf("exp_row", b)[:],
+                in_=live["q", b][:, 0:M],
+                func=ACT.Exp,
+                scale=-1.0,
+                bias=buf("min_q", b)[:],
+                accum_out=buf("total", b)[:],
+            )
+
+        def exp_own(b):
+            nc.scalar.activation(
+                out=buf("exp_own", b)[:], in_=buf("minus_q", b)[:], func=ACT.Exp, scale=-1.0, bias=buf("min_q", b)[:]
+            )
+
+        def invert_total(b):
+            nc.vector.reciprocal(out=buf("inverse_total", b)[:], in_=buf("total", b)[:])
+
+        def alpha(kind, b):
+            nc.vector.tensor_scalar(
+                out=buf("alpha_" + kind, b)[:],
+                in0=buf("exp_" + kind, b)[:],
+                scalar1=buf("inverse_total", b)[:],
+                scalar2=float(M),
+                op0=ALU.mult,
+                op1=ALU.mult,
+            )
+
+        def output(i, b):
+            result = buf("out", b)
+            nc.scalar.activation(
+                out=grouped_by_four(result[:, i, :].rearrange("p (m t) -> p m t", t=T)),
+                in_=by_four(live["pool%d" % i, b][:].rearrange("p (t m) -> p t m", t=T)),
+                func=ACT.Copy,
+                scale=buf("alpha_own", b)[:, i : i + 1],
+            )
+            nc.sync.dma_start(out=out_0[b, P * i : P * i + P, :], in_=result[:, i, :])
+
+
+        def pool_turned(i, b):
+            bank = new_bank("product", "pool_turned%d" % i, b)
+            for t in range(T):
+                multiply(part(bank, t), "u", t, b, part(buf("a_codes", b), i).bitcast(FP8X4), part(buf("a_scale", b), i))
+
+        def reweigh(i, b):
+            nc.vector.tensor_tensor(
+                out=grouped_by_four(buf("p_grouped", b)[:, P * i : P * i + P, :]),
+                in0=by_four(live["pool_turned%d" % i, b][:].rearrange("p (t m) -> p t m", t=T)),
+                in1=row_by_four(part(buf("alpha_row", b), i)),
+                op=ALU.mult,
+            )
+
+        def quantize_p(b):
+            quantize("p", b, part(p_scale, b, M))
+            words = part(out_1[0], b, M).rearrange("p m t -> p (m t)")
+            nc.sync.dma_start(out=words.bitcast(I32), in_=buf("p_codes", b)[:].bitcast(I32))
+            if b == B - 1:
+                for quad in range(4):
+                    nc.sync.dma_start(
+                        out=out_2[0, 4 * quad : 4 * quad + 4, :].bitcast(I32),
+                        in_=p_scale[32 * quad : 32 * quad + 4, :].bitcast(I32),
+                    )
+
+        steps = {
+            "exp": exponential, "fold_pairs": fold_pairs, "fold_all": fold_all, "sum_tokens": sum_tokens,
+            "invert_sums": invert_sums, "spread_inverse": spread_inverse, "gain": gain, "spread_q": spread_q,
+            "min_q": min_q, "exp_row": exp_row, "exp_own": exp_own, "invert_total": invert_total,
+            "alpha_own": lambda b: alpha("own", b), "alpha_row": lambda b: alpha("row", b), "quantize_p": quantize_p,
         }
+        for name in ("h", "e", "a", "u"):
+            steps["quantize_" + name] = lambda b, name=name: quantize_operand(name, b)
         for i in range(2):
-            for x in "he":
-                DO["T%s%d" % (x, i)] = lambda b, x=x, i=i: turn(x, i, b)
-                DO["X%s%d" % (x, i)] = lambda b, x=x, i=i: unload(x, i, b)
-            for name, fn in (("K", mm_k), ("H", tanh), ("A", amul), ("V", mm_v), ("D", qdot), ("O", outp), ("B", mm_b), ("C", pmul)):
-                DO["%s%d" % (name, i)] = lambda b, fn=fn, i=i: fn(i, b)
-        for q in range(4):
-            DO["U%d" % q] = lambda b, q=q: mm_u(q, b)
-            DO["Y%d" % q] = lambda b, q=q: uout(q, b)
+            for name in ("h", "e"):
+                steps["turn_%s%d" % (name, i)] = lambda b, name=name, i=i: turn(name, i, b)
+                steps["unload_%s%d" % (name, i)] = lambda b, name=name, i=i: unload_turned(name, i, b)
+            for name, step in (
+                ("score", score), ("tanh", tanh), ("weigh", weigh), ("pool", pool), ("dot", dot), ("output", output),
+                ("pool_turned", pool_turned), ("reweigh", reweigh),
+            ):
+                steps["%s%d" % (name, i)] = lambda b, step=step, i=i: step(i, b)
+        for i in range(4):
+            steps["project%d" % i] = lambda b, i=i: project(i, b)
+            steps["unload_u%d" % i] = lambda b, i=i: unload_u(i, b)
 
         with tc.manual_schedule():
-            load("h", h, 0)
-            nc.vector.memset(w1s[:].bitcast(I32), 0)
-            nc.vector.memset(wss_in[:].bitcast(I32), 0)
-            nc.gpsimd.memset(wg[:], 0.0)
+            load("h", 0)
+            nc.vector.memset(w1_scale[:].bitcast(I32), 0)
+            nc.vector.memset(ws_scale_loaded[:].bitcast(I32), 0)
+            nc.gpsimd.memset(token_rows[:], 0.0)
             nc.vector.memset(ones[:], 1.0)
-            make_identity(nc, ident[:])
-            nc.sync.dma_start(out=w1w[:].bitcast(I32), in_=w1_words[0].bitcast(I32))
-            for q in range(4):
-                nc.sync.dma_start(out=w1s[32 * q:32 * q + 4, :].bitcast(I32), in_=w1_scales[0, 4 * q:4 * q + 4, :].bitcast(I32))
-            load("e", e, 0)
-            nc.sync.dma_start(out=wsw_in[:].bitcast(I32), in_=ws_words[0].bitcast(I32))
-            load("h", h, 1)
-            nc.sync.dma_start(out=tb_sb[0:8, :], in_=tb[:, :])
-            nc.sync.dma_start(out=g_sb[0:8, :], in_=g[:, :])
-            for q in range(4):
-                nc.sync.dma_start(out=wss_in[32 * q:32 * q + 4, :].bitcast(I32), in_=ws_scales[0, 4 * q:4 * q + 4, :].bitcast(I32))
-            load("e", e, 1)
-            load("h", h, 2)
-            load("e", e, 2)
-            last = max(lag for step, lag in STEPS)
-            for n in range(B + last):
-                if 3 <= n + 3 < B:
-                    load("h", h, n + 3)
-                    load("e", e, n + 3)
+            make_identity(nc, identity[:])
+            nc.sync.dma_start(out=w1_codes[:].bitcast(I32), in_=w1_words[0].bitcast(I32))
+            load_scale(w1_scale, w1_scales)
+            load("e", 0)
+            nc.sync.dma_start(out=ws_loaded[:].bitcast(I32), in_=ws_words[0].bitcast(I32))
+            load("h", 1)
+            nc.sync.dma_start(out=tb_rows[0:B, :], in_=tb[:, :])
+            nc.sync.dma_start(out=g_rows[0:B, :], in_=g[:, :])
+            load_scale(ws_scale_loaded, ws_scales)
+            load("e", 1)
+            for b in range(2, AHEAD):
+                load("h", b)
+                load("e", b)
+            for n in range(B + max(lag for step, lag in PERIOD)):
+                if n + AHEAD < B:
+                    load("h", n + AHEAD)
+                    load("e", n + AHEAD)
                 if n == 0:
-                    nc.sync.dma_start(out=cb[:].rearrange("p b j -> p (b j)"), in_=c.rearrange("b j -> (b j)").partition_broadcast(P))
-                for step, lag in STEPS:
+                    c_row = c.rearrange("b j -> (b j)").partition_broadcast(P)
+                    nc.sync.dma_start(out=c_all[:].rearrange("p b j -> p (b j)"), in_=c_row)
+                for step, lag in PERIOD:
                     if 0 <= n - lag < B:
-                        DO[step](n - lag)
+                        steps[step](n - lag)

import math
from contextlib import ExitStack

import concourse.mybir as mybir
from concourse.masks import make_identity

B, S, D, M = 8, 512, 512, 256
P = 128
T = 4
FLOPS = 2 * B * (S * D * M + S * D * D + M * S * D)

F32 = mybir.dt.float32
BF16 = mybir.dt.bfloat16
I32 = mybir.dt.int32
U32 = mybir.dt.uint32
U8 = mybir.dt.uint8
FP8X4 = mybir.dt.float8_e4m3fn_x4
FP4X4 = mybir.dt.float4_e2m1fn_x4
ACT = mybir.ActivationFunctionType
ALU = mybir.AluOpType
AXIS_X = mybir.AxisListType.X

SUM_COLUMNS = 64
AHEAD = 3

PERIOD = (
    ("pool1", 4), ("output1", 5), ("score1", 1), ("unload_e0", 2), ("spread_inverse", 3), ("dot1", 4),
    ("turn_h0", 0), ("tanh0", 1), ("pool0", 4), ("tanh1", 1), ("weigh0", 3), ("weigh1", 3), ("project0", 3),
    ("dot0", 4), ("project2", 3), ("unload_h0", 0), ("unload_u0", 3), ("quantize_p", 5), ("quantize_e", 2),
    ("turn_h1", 0), ("unload_u2", 3), ("unload_h1", 0), ("project1", 3), ("spread_q", 4), ("project3", 3),
    ("min_q", 4), ("unload_u1", 3), ("exp_row", 4), ("fold_all", 2), ("gain", 2), ("exp_own", 4),
    ("quantize_h", 0), ("invert_total", 4), ("turn_e1", 0), ("unload_u3", 3), ("quantize_a", 3),
    ("alpha_own", 4), ("exp", 1), ("pool_turned0", 4), ("turn_e0", 1), ("pool_turned1", 4), ("alpha_row", 4),
    ("quantize_u", 3), ("reweigh1", 4), ("sum_tokens", 2), ("score0", 0), ("output0", 4), ("invert_sums", 2),
    ("reweigh0", 4), ("unload_e1", 0), ("fold_pairs", 1),
)


def tile_comireclabelawareinterests_x2_kernel(
    tc, h, w1_words, w1_scales, tb, g, e, ws_words, ws_scales, c, out_0, out_1, out_2
):
    nc = tc.nc
    source = {"h": h, "e": e}

    with ExitStack() as ctx:
        keep = ctx.enter_context(tc.tile_pool(name="keep", bufs=1))
        work = ctx.enter_context(tc.tile_pool(name="work", bufs=3))
        banks = {
            "turn": ctx.enter_context(tc.psum_pool(name="ps_turn", bufs=2)),
            "product": ctx.enter_context(tc.psum_pool(name="ps_product", bufs=3)),
            "v": ctx.enter_context(tc.psum_pool(name="ps_v", bufs=2)),
            "row": ctx.enter_context(tc.psum_pool(name="ps_row", bufs=1)),
        }

        w1_codes = keep.tile([P, 2 * M], U8, name="w1_codes", align_bytes=64)
        w1_scale = keep.tile([P, M], U8, name="w1_scale", align_bytes=64)
        ws_loaded = keep.tile([P, 2 * D], U8, name="ws_loaded", align_bytes=64)
        ws_scale_loaded = keep.tile([P, D], U8, name="ws_scale_loaded", align_bytes=64)
        ws_codes = keep.tile([P, 2 * D], U8, name="ws_codes", align_bytes=64)
        ws_scale = keep.tile([P, D], U8, name="ws_scale", align_bytes=64)
        tb_rows = keep.tile([P, S], BF16, name="tb_rows")
        g_rows = keep.tile([P, S], BF16, name="g_rows")
        token_rows = keep.tile([P, 2, S], F32, name="token_rows")
        token_cols = keep.tile([P, T, 2 * B], F32, name="token_cols")
        c_all = keep.tile([P, B, D], BF16, name="c_all")
        ones = keep.tile([P, SUM_COLUMNS], F32, name="ones")
        identity = keep.tile([P, P], F32, name="identity")
        p_scale = keep.tile([P, B * M], U8, name="p_scale", align_bytes=64)

        shapes = {
            "h": ([P, T, D], BF16, 6), "e": ([P, T, D], BF16, 6),
            "h_grouped": ([P, S, T], BF16, 3), "e_grouped": ([P, S, T], BF16, 3),
            "h_codes": ([P, S], U32, 3), "e_codes": ([P, S], U32, 3),
            "h_scale": ([P, S], U8, 3), "e_scale": ([P, S], U8, 3),
            "tanh": ([P, T, M], F32, 3), "exp": ([P, T, M], F32, 3), "gained": ([P, T, M], F32, 3),
            "pair_sum": ([P, 2, M], F32, 3), "token_sum": ([P, M], F32, 3), "inverse": ([P, 2], F32, 4),
            "a_grouped": ([P, M, T], BF16, 3), "a_codes": ([P, M], U32, 4), "a_scale": ([P, M], U8, 4),
            "u_grouped": ([P, D, T], BF16, 3), "u_codes": ([P, D], U32, 4), "u_scale": ([P, D], U8, 4),
            "minus_q": ([P, 2], F32, 4), "min_q": ([P, 1], F32, 4), "total": ([P, 1], F32, 4),
            "exp_row": ([P, M], F32, 3), "exp_own": ([P, 2], F32, 4), "inverse_total": ([P, 1], F32, 4),
            "alpha_own": ([P, 2], F32, 4), "alpha_row": ([P, M], F32, 3),
            "out": ([P, 2, D], F32, 4), "p_grouped": ([P, M, T], BF16, 3), "p_codes": ([P, M], U32, 4),
        }
        live = {}

        def buf(name, b):
            if (name, b) not in live:
                shape, dtype, bufs = shapes[name]
                live[name, b] = work.tile(shape, dtype, name=name, bufs=bufs, align_bytes=64)
            return live[name, b]

        def new_bank(kind, name, b):
            live[name, b] = banks[kind].tile([P, 512], F32, name=kind)
            return live[name, b]

        def part(ap, i, width=P):
            return ap[:, width * i : width * i + width]

        def as_words(ap):
            return ap[:].rearrange("p x y -> p (x y)").bitcast(F32)

        def by_four(ap):
            return ap.rearrange("p t (n i) -> p n t i", i=4)

        def grouped_by_four(ap):
            return ap.rearrange("p (n i) t -> p n t i", i=4)

        def row_by_four(row):
            return row.rearrange("p (n i) -> p n i", i=4).unsqueeze(2).to_broadcast([P, P // 4, T, 4])


        def load(name, b):
            tile = buf(name, b)
            rows = source[name][b].rearrange("(p t) f -> p t f", t=T)
            pieces = 2 if b == 0 else 1
            for i in range(pieces):
                ts = slice(i * T // pieces, (i + 1) * T // pieces)
                nc.sync.dma_start(out=tile[:, ts, :], in_=rows[:, ts, :])

        def load_scale(tile, scales):
            for quad in range(4):
                nc.sync.dma_start(
                    out=tile[32 * quad : 32 * quad + 4, :].bitcast(I32),
                    in_=scales[0, 4 * quad : 4 * quad + 4, :].bitcast(I32),
                )

        def token_columns():
            largest = work.tile([P, 1], F32, name="largest", bufs=1)
            nc.vector.tensor_reduce(out=largest[0:B, :], in_=tb_rows[0:B, :], axis=AXIS_X, op=ALU.max)
            shift = work.tile([P, 1], F32, name="shift", bufs=1)
            nc.vector.tensor_scalar(
                out=shift[0:B, :], in0=largest[0:B, :], scalar1=-1.0, scalar2=-2.0, op0=ALU.mult, op1=ALU.add
            )
            nc.vector.tensor_scalar(
                out=token_rows[0:B, 0, :], in0=tb_rows[0:B, :], scalar1=shift[0:B, :], scalar2=None, op0=ALU.add
            )
            nc.vector.tensor_scalar(
                out=token_rows[0:B, 1, :], in0=g_rows[0:B, :], scalar1=math.sqrt(S), scalar2=None, op0=ALU.mult
            )
            for r in range(2):
                bank = new_bank("turn", "token_rows", r)
                for t in range(T):
                    nc.tensor.transpose(part(bank, t), token_rows[:, r, t : t + S - T + 1 : T], identity[:])
                nc.vector.tensor_copy(
                    out=token_cols[:, :, B * r : B * r + B],
                    in_=bank[:].rearrange("p (t n) -> p t n", t=T)[:, :, 0:B],
                )

        def permute_ws():
            nc.vector.tensor_copy(
                out=ws_scale[:].rearrange("p (t m) -> p m t", t=T),
                in_=ws_scale_loaded[:].rearrange("p (m t) -> p m t", t=T),
            )
            nc.vector.tensor_copy(
                out=ws_codes[:].rearrange("p (t m y) -> p m t y", t=T, y=2),
                in_=ws_loaded[:].rearrange("p (m t y) -> p m t y", t=T, y=2),
            )


        def turn(name, half, b):
            bank = new_bank("turn", "turn_%s%d" % (name, half), b)
            words = as_words(buf(name, b))
            for tt in range(2):
                for y in range(2):
                    first = (2 * half + tt) * (D // 2) + y
                    nc.tensor.transpose(part(bank, 2 * tt + y), words[:, first : first + D // 2 - 1 : 2], identity[:])

        def unload_turned(name, half, b):
            words = as_words(buf(name + "_grouped", b)).rearrange("p (s y) -> p s y", y=2)
            nc.scalar.copy(
                out=words[:, 2 * P * half : 2 * P * half + 2 * P, :].rearrange("p (t r) y -> p t r y", t=2),
                in_=live["turn_%s%d" % (name, half), b][:].rearrange("p (t y r) -> p t r y", t=2, y=2),
            )

        def quantize(name, b, scale):
            nc.vector.quantize_mx(
                out=buf(name + "_codes", b)[:].bitcast(FP8X4),
                scales=scale,
                in_=buf(name + "_grouped", b)[:].rearrange("p n t -> p (n t)"),
            )

        def quantize_operand(name, b):
            quantize(name, b, buf(name + "_scale", b)[:])
            if name == "e" and b == 0:
                permute_ws()

        def multiply(out, name, i, b, rhs, rhs_scale):
            nc.tensor.matmul_mx(
                out=out,
                lhsT=part(buf(name + "_codes", b), i).bitcast(FP8X4),
                lhsT_scale=part(buf(name + "_scale", b), i),
                rhs=rhs,
                rhs_scale=rhs_scale,
                start=True,
                stop=True,
            )


        def score(half, b):
            bank = new_bank("product", "score%d" % half, b)
            for tt in range(2):
                multiply(part(bank, tt, M), "h", 2 * half + tt, b, w1_codes[:].bitcast(FP4X4), w1_scale[:])

        def tanh(half, b):
            nc.scalar.activation(
                out=buf("tanh", b)[:, 2 * half : 2 * half + 2, :],
                in_=live["score%d" % half, b][:].rearrange("p (t m) -> p t m", t=2),
                func=ACT.Tanh,
            )

        def exponential(b):
            if b == 0:
                token_columns()
            for t in range(T):
                nc.scalar.activation(
                    out=buf("exp", b)[:, t, :],
                    in_=buf("tanh", b)[:, t, :],
                    func=ACT.Exp,
                    scale=2.0,
                    bias=token_cols[:, t, b : b + 1],
                )

        def fold_pairs(b):
            x = buf("exp", b)
            nc.vector.tensor_tensor(out=buf("pair_sum", b)[:], in0=x[:, 0:2, :], in1=x[:, 2:4, :], op=ALU.add)

        def fold_all(b):
            x = buf("pair_sum", b)
            nc.vector.tensor_tensor(out=buf("token_sum", b)[:], in0=x[:, 0, :], in1=x[:, 1, :], op=ALU.add)

        def sum_tokens(b):
            bank = new_bank("row", "sums", b)
            for i in range(2):
                nc.tensor.matmul(
                    part(bank, i, SUM_COLUMNS), lhsT=part(buf("token_sum", b), i), rhs=ones[:], start=True, stop=True
                )

        def invert_sums(b):
            first_columns = live["sums", b][:, 0 : SUM_COLUMNS + 1 : SUM_COLUMNS]
            nc.vector.reciprocal(out=buf("inverse", b)[:], in_=first_columns)

        def spread(bank, first, column_pair):
            for i in range(2):
                nc.tensor.transpose(
                    part(bank, first + i), column_pair[:, i : i + 1].to_broadcast([P, P]), identity[:]
                )

        def spread_inverse(b):
            spread(live["sums", b], 2, buf("inverse", b))

        def gain(b):
            for t in range(T):
                nc.vector.tensor_scalar(
                    out=buf("gained", b)[:, t, :],
                    in0=buf("exp", b)[:, t, :],
                    scalar1=token_cols[:, t, B + b : B + b + 1],
                    scalar2=None,
                    op0=ALU.mult,
                )

        def weigh(i, b):
            ms = slice(P * i, P * i + P)
            nc.vector.tensor_tensor(
                out=grouped_by_four(buf("a_grouped", b)[:, ms, :]),
                in0=by_four(buf("gained", b)[:, :, ms]),
                in1=row_by_four(part(live["sums", b], 2 + i)),
                op=ALU.mult,
            )


        def project(i, b):
            bank = new_bank("product", "project%d" % i, b)
            for t in range(T):
                multiply(part(bank, t), "e", t, b, part(ws_codes, i, 2 * P).bitcast(FP4X4), part(ws_scale, i))

        def unload_u(i, b):
            nc.scalar.copy(
                out=grouped_by_four(buf("u_grouped", b)[:, P * i : P * i + P, :]),
                in_=by_four(live["project%d" % i, b][:].rearrange("p (t n) -> p t n", t=T)),
            )


        def pool(i, b):
            bank = new_bank("v", "pool%d" % i, b)
            multiply(bank[:], "a", i, b, buf("u_codes", b)[:].bitcast(FP8X4), buf("u_scale", b)[:])

        def dot(i, b):
            products = work.tile([P, D], F32, name="products", bufs=2, align_bytes=64)
            nc.vector.scalar_tensor_tensor(
                out=products[:].rearrange("p (t m) -> p t m", t=T),
                in0=live["pool%d" % i, b][:].rearrange("p (t m) -> p t m", t=T),
                scalar=-1.0 / math.sqrt(D),
                in1=c_all[:, b, :].rearrange("p (m t) -> p t m", t=T),
                op0=ALU.mult,
                op1=ALU.mult,
                accum_out=buf("minus_q", b)[:, i : i + 1],
            )

        def spread_q(b):
            spread(new_bank("row", "q", b), 0, buf("minus_q", b))

        def min_q(b):
            nc.vector.tensor_reduce(out=buf("min_q", b)[:], in_=live["q", b][:, 0:M], axis=AXIS_X, op=ALU.min)

        def exp_row(b):
            nc.scalar.activation(
                out=buf("exp_row", b)[:],
                in_=live["q", b][:, 0:M],
                func=ACT.Exp,
                scale=-1.0,
                bias=buf("min_q", b)[:],
                accum_out=buf("total", b)[:],
            )

        def exp_own(b):
            nc.scalar.activation(
                out=buf("exp_own", b)[:], in_=buf("minus_q", b)[:], func=ACT.Exp, scale=-1.0, bias=buf("min_q", b)[:]
            )

        def invert_total(b):
            nc.vector.reciprocal(out=buf("inverse_total", b)[:], in_=buf("total", b)[:])

        def alpha(kind, b):
            nc.vector.tensor_scalar(
                out=buf("alpha_" + kind, b)[:],
                in0=buf("exp_" + kind, b)[:],
                scalar1=buf("inverse_total", b)[:],
                scalar2=float(M),
                op0=ALU.mult,
                op1=ALU.mult,
            )

        def output(i, b):
            result = buf("out", b)
            nc.scalar.activation(
                out=grouped_by_four(result[:, i, :].rearrange("p (m t) -> p m t", t=T)),
                in_=by_four(live["pool%d" % i, b][:].rearrange("p (t m) -> p t m", t=T)),
                func=ACT.Copy,
                scale=buf("alpha_own", b)[:, i : i + 1],
            )
            nc.sync.dma_start(out=out_0[b, P * i : P * i + P, :], in_=result[:, i, :])


        def pool_turned(i, b):
            bank = new_bank("product", "pool_turned%d" % i, b)
            for t in range(T):
                multiply(part(bank, t), "u", t, b, part(buf("a_codes", b), i).bitcast(FP8X4), part(buf("a_scale", b), i))

        def reweigh(i, b):
            nc.vector.tensor_tensor(
                out=grouped_by_four(buf("p_grouped", b)[:, P * i : P * i + P, :]),
                in0=by_four(live["pool_turned%d" % i, b][:].rearrange("p (t m) -> p t m", t=T)),
                in1=row_by_four(part(buf("alpha_row", b), i)),
                op=ALU.mult,
            )

        def quantize_p(b):
            quantize("p", b, part(p_scale, b, M))
            words = part(out_1[0], b, M).rearrange("p m t -> p (m t)")
            nc.sync.dma_start(out=words.bitcast(I32), in_=buf("p_codes", b)[:].bitcast(I32))
            if b == B - 1:
                for quad in range(4):
                    nc.sync.dma_start(
                        out=out_2[0, 4 * quad : 4 * quad + 4, :].bitcast(I32),
                        in_=p_scale[32 * quad : 32 * quad + 4, :].bitcast(I32),
                    )

        steps = {
            "exp": exponential, "fold_pairs": fold_pairs, "fold_all": fold_all, "sum_tokens": sum_tokens,
            "invert_sums": invert_sums, "spread_inverse": spread_inverse, "gain": gain, "spread_q": spread_q,
            "min_q": min_q, "exp_row": exp_row, "exp_own": exp_own, "invert_total": invert_total,
            "alpha_own": lambda b: alpha("own", b), "alpha_row": lambda b: alpha("row", b), "quantize_p": quantize_p,
        }
        for name in ("h", "e", "a", "u"):
            steps["quantize_" + name] = lambda b, name=name: quantize_operand(name, b)
        for i in range(2):
            for name in ("h", "e"):
                steps["turn_%s%d" % (name, i)] = lambda b, name=name, i=i: turn(name, i, b)
                steps["unload_%s%d" % (name, i)] = lambda b, name=name, i=i: unload_turned(name, i, b)
            for name, step in (
                ("score", score), ("tanh", tanh), ("weigh", weigh), ("pool", pool), ("dot", dot), ("output", output),
                ("pool_turned", pool_turned), ("reweigh", reweigh),
            ):
                steps["%s%d" % (name, i)] = lambda b, step=step, i=i: step(i, b)
        for i in range(4):
            steps["project%d" % i] = lambda b, i=i: project(i, b)
            steps["unload_u%d" % i] = lambda b, i=i: unload_u(i, b)

        with tc.manual_schedule():
            load("h", 0)
            nc.vector.memset(w1_scale[:].bitcast(I32), 0)
            nc.vector.memset(ws_scale_loaded[:].bitcast(I32), 0)
            nc.gpsimd.memset(token_rows[:], 0.0)
            nc.vector.memset(ones[:], 1.0)
            make_identity(nc, identity[:])
            nc.sync.dma_start(out=w1_codes[:].bitcast(I32), in_=w1_words[0].bitcast(I32))
            load_scale(w1_scale, w1_scales)
            load("e", 0)
            nc.sync.dma_start(out=ws_loaded[:].bitcast(I32), in_=ws_words[0].bitcast(I32))
            load("h", 1)
            nc.sync.dma_start(out=tb_rows[0:B, :], in_=tb[:, :])
            nc.sync.dma_start(out=g_rows[0:B, :], in_=g[:, :])
            load_scale(ws_scale_loaded, ws_scales)
            load("e", 1)
            for b in range(2, AHEAD):
                load("h", b)
                load("e", b)
            for n in range(B + max(lag for step, lag in PERIOD)):
                if n + AHEAD < B:
                    load("h", n + AHEAD)
                    load("e", n + AHEAD)
                if n == 0:
                    c_row = c.rearrange("b j -> (b j)").partition_broadcast(P)
                    nc.sync.dma_start(out=c_all[:].rearrange("p b j -> p (b j)"), in_=c_row)
                for step, lag in PERIOD:
                    if 0 <= n - lag < B:
                        steps[step](n - lag)
